import numpy as np
import ml_dtypes


def mxq(x, axis, fmt="e4m3"):
    dtype, down = {"e4m3": (ml_dtypes.float8_e4m3fn, 7), "e5m2": (ml_dtypes.float8_e5m2, 14)}[fmt]
    v = np.moveaxis(np.asarray(x, np.float32).astype(ml_dtypes.bfloat16).astype(np.float64), axis, -1)
    blocks = v.reshape(v.shape[:-1] + (-1, 32))
    amax = np.abs(blocks).max(-1, keepdims=True)
    byte = np.maximum(np.where(amax > 0, np.frexp(amax)[1] - 1 + 127, 0) - down, 1)
    scale = np.exp2(byte - 127.0)
    codes = (blocks / scale).astype(np.float32).astype(dtype).astype(np.float64)
    return np.moveaxis((codes * scale).reshape(v.shape), -1, axis)


WIDE = False


def mx_kscale(k):
    if not WIDE:
        return np.ones(k)
    levels = np.array([10, -10, 5, -5, 0])
    if k % 512:
        return np.exp2(np.random.permutation(np.resize(levels, k // 32))).repeat(32)
    a = np.empty((k // 512, 16))
    for p in range(k // 512):
        a[p, :8] = np.random.permutation(np.resize(levels, 8))
        for g in range(8):
            far = levels[np.abs(levels - a[p, g]) >= 10]
            a[p, g + 8] = far[np.random.randint(len(far))]
    return np.exp2(a.ravel()).repeat(32)


BF16 = ml_dtypes.bfloat16


def bf(x):
    return np.asarray(x, np.float32).astype(BF16)


def f64(x):
    return np.asarray(x).astype(np.float64)


E2M1 = np.array([0.0, 0.5, 1.0, 1.5, 2.0, 3.0, 4.0, 6.0, -0.0, -0.5, -1.0, -1.5, -2.0, -3.0, -4.0, -6.0])


def pack_weight(w, fmt):
    k, n = w.shape
    w = f64(bf(w)).reshape(k // 32, 32, n)
    amax = np.abs(w).max(1)
    if fmt == "e4m3":
        byte = np.frexp(amax)[1] - 1 + 127 - 7
    else:
        mant, ex = np.frexp(amax / 6.0)
        byte = np.where(mant > 0.5, ex, ex - 1) + 127
    byte = np.clip(np.where(amax > 0, byte, 1), 1, 254)
    scaled = (w * np.exp2(127.0 - byte)[:, None, :]).reshape(k, n).astype(np.float32)
    by_word = np.ascontiguousarray(scaled.reshape(k // 512, 128, 4, n).transpose(0, 1, 3, 2))
    if fmt == "e4m3":
        words = by_word.astype(ml_dtypes.float8_e4m3fn).view(np.uint8)
    else:
        c = by_word.astype(ml_dtypes.float4_e2m1fn).view(np.uint8) & 0xF
        words = c[..., 0::2] | (c[..., 1::2] << 4)
    return np.ascontiguousarray(words), np.ascontiguousarray(byte.astype(np.uint8).reshape(k // 512, 16, n))


def unpack_weight(words, scales, fmt):
    g, p, n, _ = words.shape
    if fmt == "e4m3":
        vals = np.ascontiguousarray(words).view(ml_dtypes.float8_e4m3fn).astype(np.float64)
    else:
        nib = np.empty((g, p, n, 4), np.uint8)
        nib[..., 0::2] = words & 0xF
        nib[..., 1::2] = words >> 4
        vals = E2M1[nib]
    vals = vals * np.repeat(np.exp2(scales.astype(np.float64) - 127.0), 8, axis=1)[..., None]
    return vals.transpose(0, 1, 3, 2).reshape(g * 512, n)
def pack4(w):
    words, scales = pack_weight(w, "e2m1")
    return words.reshape(words.shape[0], 128, -1), scales


def unpack4(words, scales):
    return unpack_weight(words.reshape(words.shape[0], 128, -1, 2), scales, "e2m1")


def planes(Y):
    n, m = Y.shape
    b = f64(bf(Y)).reshape(n // 32, 32, m)
    amax = np.abs(b).max(1)
    byte = np.clip(np.where(amax > 0, np.frexp(amax)[1] - 1 + 127 - 7, 1), 1, 254)
    codes = (b * np.exp2(127.0 - byte)[:, None, :]).reshape(n, m).astype(np.float32).astype(ml_dtypes.float8_e4m3fn).view(np.uint8)
    words = codes.reshape(n // 512, 128, 4, m).transpose(0, 1, 3, 2)
    return np.ascontiguousarray(words), np.ascontiguousarray(byte.astype(np.uint8).reshape(n // 512, 16, m))


S, P, K, R, Q = 1024, 2, 512, 1024, 1536
R_MIN, R_MAX = 2.0, 40.0
Q_MIN, Q_MAX = 1.5, 18.0

def jittered_grid(lo, hi, n):
    return lo + (hi - lo) * (np.arange(n) + np.random.rand(n)) / n

def setup_inputs():
    rn = np.random.randn
    s, t = mx_kscale(K), mx_kscale(R)
    tt = np.tile(t, P)
    dist, qv = jittered_grid(R_MIN, R_MAX, R), jittered_grid(Q_MIN, Q_MAX, Q)
    shell = np.tile(2.0 * dist / dist.mean(), P)
    coef_words, coef_scales = pack4(rn(K, S) * s[:, None])
    modes_words, modes_scales = pack4(rn(K, P * R) * shell * tt / np.sqrt(K) / s[:, None])
    gain = bf(1 + 0.1 * rn(P * R))
    base = bf(0.5 * rn(P * R) * shell * tt)
    x = dist[:, None] * qv[None, :]
    sinc = bf(np.sin(x) / x / t[:, None])
    form = bf(qv * dist.mean() / (2.0 * np.sqrt(R)) * np.exp(0.6 * rn(P, Q)))
    selfscat = bf(0.5 * np.exp(0.6 * rn(Q)))
    return dict(coef_words=coef_words, coef_scales=coef_scales, modes_words=modes_words,
                modes_scales=modes_scales, gain=gain, base=base, sinc=sinc, form=form, selfscat=selfscat)

def reference(coef_words, coef_scales, modes_words, modes_scales, gain, base, sinc, form, selfscat):
    C, D = unpack4(coef_words, coef_scales), unpack4(modes_words, modes_scales)
    H = C.T @ D
    h = (H * f64(gain) + f64(base)).reshape(S * P, R)
    part = (mxq(h, 1, "e4m3") @ mxq(f64(sinc), 0, "e4m3")).reshape(S, P, Q)
    w = f64(form)
    y = part[:, 0] * w[0] + part[:, 1] * w[1] + f64(selfscat)
    Y = y.T
    words, scales = planes(Y)
    return y, words, scales

@@ -1,0 +1,383 @@
+from contextlib import ExitStack
+
+import concourse.mybir as mybir
+from concourse.masks import make_identity
+
+S, KINDS, MODES, R, Q = 1024, 2, 512, 1024, 1536
+FLOPS = 2 * S * MODES * KINDS * R + 2 * S * KINDS * R * Q
+
+F32 = mybir.dt.float32
+BF16 = mybir.dt.bfloat16
+I32 = mybir.dt.int32
+U32 = mybir.dt.uint32
+U8 = mybir.dt.uint8
+FP8X4 = mybir.dt.float8_e4m3fn_x4
+FP4X4 = mybir.dt.float4_e2m1fn_x4
+IDENT = mybir.ActivationFunctionType.Identity
+MULT = mybir.AluOpType.mult
+ADD = mybir.AluOpType.add
+
+P = 128
+T = 4
+W = 512
+CHUNKS = S // W
+DG = R // W
+CG = Q // W
+ROW_GAIN, ROW_BASE, D_ROWS = 0, 4, 8
+ROW_FORM, ROW_SELF, C_ROWS = 0, 6, 9
+
+
+def tile_powder_pattern_sinc_k5_kernel(
+    tc, coef_words, coef_scales, modes_words, modes_scales, gain, base, sinc, form, selfscat, out_0, out_1, out_2
+):
+    nc = tc.nc
+    with ExitStack() as ctx:
+        keep = ctx.enter_context(tc.tile_pool(name="keep", bufs=1))
+        work = ctx.enter_context(tc.tile_pool(name="work", bufs=2))
+        psum = ctx.enter_context(tc.psum_pool(name="psum", bufs=1))
+        ctx.enter_context(tc.manual_schedule())
+
+        def bank(n):
+            return psum.tile([P, W], F32, name="bank", bufs=8)
+
+        c_words = keep.tile([P, 2 * S], U8, align_bytes=64)
+        c_scales = keep.tile([P, S], U8, align_bytes=64)
+        d_words_in = keep.tile([P, 2 * KINDS * R], U8, align_bytes=64)
+        d_scales_in = keep.tile([P, KINDS * R], U8, align_bytes=64)
+        d_words = keep.tile([P, 2 * KINDS * R], U8, align_bytes=64)
+        d_scales = keep.tile([P, KINDS * R], U8, align_bytes=64)
+        sinc_in = keep.tile([P, CG, DG, T, W], BF16, align_bytes=64)
+        sinc_codes = keep.tile([P, CG, DG, W], U32, align_bytes=64)
+        sinc_scales = keep.tile([P, CG, DG, W], U8, align_bytes=64)
+        h_codes = keep.tile([P, CHUNKS, KINDS * DG, W], U32, align_bytes=64)
+        h_scales = keep.tile([P, CHUNKS, KINDS * DG, W], U8, align_bytes=64)
+        y_scales = keep.tile([P, CG, S], U8, align_bytes=64)
+        d_vec_in = keep.tile([P, W], BF16, align_bytes=64)
+        c_vec_in = keep.tile([P, W], BF16, align_bytes=64)
+        d_rows = keep.tile([P, T, P], F32, align_bytes=64)
+        c_rows = keep.tile([P, T, P], F32, align_bytes=64)
+        d_vec = keep.tile([P, T, D_ROWS], F32, align_bytes=64)
+        c_vec = keep.tile([P, T, C_ROWS], F32, align_bytes=64)
+        ident = keep.tile([P, P], F32, align_bytes=64)
+
+        nc.vector.memset(d_scales_in[:].bitcast(I32), 0)
+        nc.vector.memset(c_scales[:].bitcast(I32), 0)
+        nc.vector.memset(d_rows[:], 0.0)
+        make_identity(nc, ident[:])
+        nc.gpsimd.dma_start(out=c_vec_in[ROW_FORM:ROW_SELF, :], in_=form.rearrange("a (g n) -> (a g) n", n=W))
+        nc.gpsimd.dma_start(out=c_vec_in[ROW_SELF:C_ROWS, :], in_=selfscat.rearrange("(g n) -> g n", n=W))
+        nc.vector.memset(c_rows[:], 0.0)
+
+        def load_words(dst, src, lo, hi):
+            nc.sync.dma_start(out=dst[:, lo:hi].bitcast(I32), in_=src[0, :, lo:hi].bitcast(I32))
+
+        def load_sinc(cg, g):
+            rows = sinc[W * g : W * (g + 1), W * cg : W * (cg + 1)].rearrange("(q t r) c -> t q r c", t=T, r=8)
+            for t in range(T):
+                nc.sync.dma_start(out=sinc_in[:, cg, g, t, :], in_=rows[t])
+
+        load_words(d_words_in, modes_words, 0, 2 * R)
+        load_words(c_words, coef_words, 0, 2 * W)
+        nc.sync.dma_start(out=d_vec_in[ROW_GAIN:ROW_BASE, :], in_=gain.rearrange("(j n) -> j n", n=W))
+        nc.sync.dma_start(out=d_vec_in[ROW_BASE:D_ROWS, :], in_=base.rearrange("(j n) -> j n", n=W))
+        for quad in range(4):
+            nc.sync.dma_start(
+                out=d_scales_in[32 * quad : 32 * quad + 4, :].bitcast(I32),
+                in_=modes_scales[0, 4 * quad : 4 * quad + 4, :].bitcast(I32),
+            )
+        for quad in range(4):
+            nc.sync.dma_start(
+                out=c_scales[32 * quad : 32 * quad + 4, :].bitcast(I32),
+                in_=coef_scales[0, 4 * quad : 4 * quad + 4, :].bitcast(I32),
+            )
+        load_sinc(0, 0)
+        load_words(d_words_in, modes_words, 2 * R, 4 * R)
+        load_sinc(0, 1)
+        load_words(c_words, coef_words, 2 * W, 4 * W)
+        for cg in range(1, CG):
+            for g in range(DG):
+                load_sinc(cg, g)
+
+        def turn_vectors(rows, vec, bank_no):
+            ps = bank(bank_no)
+            for t in range(T):
+                nc.tensor.transpose(ps[:, P * t : P * (t + 1)], rows[:, t, :], ident[:])
+            nc.scalar.activation(
+                out=vec[:], in_=ps[:].rearrange("p (t j) -> p t j", t=T)[:, :, 0 : vec.shape[2]], func=IDENT
+            )
+
+        nc.scalar.activation(
+            out=d_rows[0:D_ROWS, :, :].rearrange("j t (q r) -> j t q r", r=8),
+            in_=d_vec_in[0:D_ROWS, :].rearrange("j (q t r) -> j t q r", t=T, r=8),
+            func=IDENT,
+        )
+        turn_vectors(d_rows, d_vec, 0)
+
+        def order_modes(j):
+            nc.vector.tensor_copy(
+                out=d_words[:, 2 * W * j : 2 * W * (j + 1)].bitcast(I32).rearrange("p (t q w) -> p t q w", t=T, w=4),
+                in_=d_words_in[:, 2 * W * j : 2 * W * (j + 1)].bitcast(I32).rearrange("p (q t w) -> p t q w", t=T, w=4),
+            )
+            nc.vector.tensor_copy(
+                out=d_scales[:, W * j : W * (j + 1)].bitcast(I32).rearrange("p (t q w) -> p t q w", t=T, w=2),
+                in_=d_scales_in[:, W * j : W * (j + 1)].bitcast(I32).rearrange("p (q t w) -> p t q w", t=T, w=2),
+            )
+
+        h_ps, h_rows, h_packed, sinc_packed = {}, {}, {}, {}
+        part, first_term, y_rows, y_packed, turned = {}, {}, {}, {}, {}
+
+        def weights_pass(ch, j, t, bank_no):
+            h_ps[ch, j, t] = bank(bank_no)
+            col = W * j + P * t
+            nc.tensor.matmul_mx(
+                out=h_ps[ch, j, t][:],
+                lhsT=d_words[:, 2 * col : 2 * (col + P)].bitcast(FP4X4),
+                lhsT_scale=d_scales[:, col : col + P],
+                rhs=c_words[:, 2 * W * ch : 2 * W * (ch + 1)].bitcast(FP4X4),
+                rhs_scale=c_scales[:, W * ch : W * (ch + 1)],
+                start=True,
+                stop=True,
+            )
+            if t == 0:
+                h_rows[ch, j] = work.tile([P, T, W], BF16, name="h_rows", align_bytes=64, bufs=4)
+
+        def correct_weights(ch, j, t, on_vector):
+            gain_col = d_vec[:, t, ROW_GAIN + j : ROW_GAIN + j + 1]
+            base_col = d_vec[:, t, ROW_BASE + j : ROW_BASE + j + 1]
+            if on_vector:
+                nc.vector.tensor_scalar(h_rows[ch, j][:, t, :], h_ps[ch, j, t][:], gain_col, base_col, MULT, ADD)
+            else:
+                nc.scalar.activation(
+                    out=h_rows[ch, j][:, t, :], in_=h_ps[ch, j, t][:], func=IDENT, scale=gain_col, bias=base_col
+                )
+
+        def interleave(dst, src):
+            nc.vector.tensor_copy(
+                out=dst.rearrange("p (c i) t -> p c t i", i=4), in_=src.rearrange("p t (c i) -> p c t i", i=4)
+            )
+
+        def pack_h(ch, j):
+            h_packed[ch, j] = work.tile([P, W, T], BF16, name="packed", align_bytes=64, bufs=3)
+            interleave(h_packed[ch, j][:], h_rows[ch, j][:])
+
+        def quantize_h(ch, j):
+            nc.vector.quantize_mx(
+                out=h_codes[:, ch, j, :].bitcast(FP8X4),
+                scales=h_scales[:, ch, j, :],
+                in_=h_packed[ch, j][:].rearrange("p i t -> p (i t)"),
+            )
+
+        def pack_sinc(cg, g):
+            sinc_packed[cg, g] = work.tile([P, W, T], BF16, name="packed", align_bytes=64, bufs=3)
+            nc.vector.tensor_copy(
+                out=sinc_packed[cg, g][:].rearrange("p (u m) t -> p m t u", u=T),
+                in_=sinc_in[:, cg, g, :, :].rearrange("p t (m u) -> p m t u", u=T),
+            )
+
+        def quantize_sinc(cg, g):
+            nc.vector.quantize_mx(
+                out=sinc_codes[:, cg, g, :].bitcast(FP8X4),
+                scales=sinc_scales[:, cg, g, :],
+                in_=sinc_packed[cg, g][:].rearrange("p c t -> p (c t)"),
+            )
+
+        def partial_pattern(grp, u, a):
+            first, n, cg = grp
+            ch, lo = divmod(first, W)
+            part[grp, u, a] = bank(u)
+            for g in range(DG):
+                nc.tensor.matmul_mx(
+                    out=part[grp, u, a][:, 0:n],
+                    lhsT=sinc_codes[:, cg, g, P * u : P * (u + 1)].bitcast(FP8X4),
+                    lhsT_scale=sinc_scales[:, cg, g, P * u : P * (u + 1)],
+                    rhs=h_codes[:, ch, DG * a + g, lo : lo + n].bitcast(FP8X4),
+                    rhs_scale=h_scales[:, ch, DG * a + g, lo : lo + n],
+                    start=(g == 0),
+                    stop=(g == DG - 1),
+                )
+
+        def kind0(grp, u):
+            first, n, cg = grp
+            partial_pattern(grp, u, 0)
+            first_term[grp, u] = work.tile([P, W], F32, name="first_term", align_bytes=64, bufs=4)
+            nc.scalar.activation(
+                out=first_term[grp, u][:, 0:n],
+                in_=part[grp, u, 0][:, 0:n],
+                func=IDENT,
+                scale=c_vec[:, u, ROW_FORM + cg : ROW_FORM + cg + 1],
+                bias=c_vec[:, u, ROW_SELF + cg : ROW_SELF + cg + 1],
+            )
+
+        def kind1(grp, u):
+            first, n, cg = grp
+            partial_pattern(grp, u, 1)
+            if u == 0:
+                y_rows[grp] = work.tile([P, T, W], F32, name="y_rows", align_bytes=64, bufs=6)
+            nc.vector.scalar_tensor_tensor(
+                out=y_rows[grp][:, u, 0:n],
+                in0=part[grp, u, 1][:, 0:n],
+                scalar=c_vec[:, u, ROW_FORM + CG + cg : ROW_FORM + CG + cg + 1],
+                in1=first_term[grp, u][:, 0:n],
+                op0=MULT,
+                op1=ADD,
+            )
+
+        def pack_y(grp):
+            first, n, cg = grp
+            y_packed[grp] = work.tile([P, W, T], BF16, name="packed", align_bytes=64, bufs=3)
+            interleave(y_packed[grp][:, 0:n, :], y_rows[grp][:, :, 0:n])
+
+        def quantize_y(grp):
+            first, n, cg = grp
+            y_codes = work.tile([P, W], U32, name="y_codes", align_bytes=64, bufs=3)
+            nc.vector.quantize_mx(
+                out=y_codes[:, 0:n].bitcast(FP8X4),
+                scales=y_scales[:, cg, first : first + n],
+                in_=y_packed[grp][:, 0:n, :].rearrange("p i t -> p (i t)"),
+            )
+            nc.sync.dma_start(
+                out=out_1[cg, :, first : first + n, :].rearrange("p m t -> p (m t)").bitcast(I32),
+                in_=y_codes[:, 0:n].bitcast(I32),
+            )
+
+        def store_y_scales(cg_lo, cg_hi):
+            for quad in range(4):
+                nc.sync.dma_start(
+                    out=out_2[cg_lo:cg_hi, 4 * quad : 4 * quad + 4, :].rearrange("g r m -> r g m").bitcast(I32),
+                    in_=y_scales[32 * quad : 32 * quad + 4, cg_lo:cg_hi, :].bitcast(I32),
+                )
+
+        def turn_y(grp, blocks, banks, slots):
+            for b, bank_no in zip(blocks, banks):
+                if slots[0] == 0:
+                    turned[grp, b] = bank(bank_no)
+                for u in slots:
+                    nc.tensor.transpose(
+                        turned[grp, b][:, P * u : P * (u + 1)], y_rows[grp][:, u, P * b : P * (b + 1)], ident[:]
+                    )
+
+        def store_y(grp, b, on_vector=False):
+            first, n, cg = grp
+            y_out = work.tile([P, W], F32, name="y_out", align_bytes=64, bufs=6)
+            dst = y_out[:].rearrange("i (m u) -> i m u", u=T)
+            src = turned[grp, b][:].rearrange("i (u m) -> i m u", u=T)
+            if on_vector:
+                nc.vector.tensor_copy(out=dst, in_=src)
+            else:
+                nc.scalar.copy(out=dst, in_=src)
+            nc.sync.dma_start(out=out_0[first + P * b : first + P * (b + 1), W * cg : W * (cg + 1)], in_=y_out[:])
+
+        groups = [(W * ch, W, cg) for ch in range(CHUNKS) for cg in range(CG)]
+        groups = groups[:-1] + [(W, W // 2, CG - 1), (W + W // 2, W // 2, CG - 1)]
+        ALL = (0, 1, 2, 3)
+
+        order_modes(0)
+        order_modes(1)
+        pack_sinc(0, 0)
+        order_modes(2)
+        order_modes(3)
+        for j in range(KINDS * DG):
+            for t in range(T):
+                weights_pass(0, j, t, 4 + t)
+                correct_weights(0, j, t, False)
+            if j == 0:
+                nc.scalar.activation(
+                    out=c_rows[0:C_ROWS, :, :], in_=c_vec_in[0:C_ROWS, :].rearrange("j (m t) -> j t m", t=T), func=IDENT
+                )
+            if j == 1:
+                turn_vectors(c_rows, c_vec, 1)
+        quantize_sinc(0, 0)
+        pack_sinc(0, 1)
+        pack_h(0, 0)
+        quantize_sinc(0, 1)
+        quantize_h(0, 0)
+        pack_h(0, 1)
+        quantize_h(0, 1)
+        pack_h(0, 2)
+        for u in range(T):
+            kind0(groups[0], u)
+        quantize_h(0, 2)
+        pack_h(0, 3)
+        quantize_h(0, 3)
+        pack_sinc(1, 0)
+
+        def second_chunk_passes(j, slots):
+            for t in slots:
+                weights_pass(1, j, t, 4 + t % 2)
+                correct_weights(1, j, t, False)
+
+        def kind0_all(grp):
+            for u in range(T):
+                kind0(grp, u)
+
+        def kind1_all(grp):
+            for u in range(T):
+                kind1(grp, u)
+
+        def turn_and_store(grp, blocks, banks):
+            turn_y(grp, blocks, banks, ALL)
+            for b in blocks:
+                store_y(grp, b)
+
+        second_chunk_passes(0, (0, 1))
+        kind1(groups[0], 0)
+        quantize_sinc(1, 0)
+        kind1(groups[0], 1)
+        second_chunk_passes(0, (2, 3))
+        pack_sinc(1, 1)
+        kind1(groups[0], 2)
+        quantize_sinc(1, 1)
+        kind1(groups[0], 3)
+        second_chunk_passes(1, ALL)
+        pack_sinc(2, 0)
+        pack_h(1, 0)
+        quantize_sinc(2, 0)
+        quantize_h(1, 0)
+        kind0_all(groups[1])
+        turn_and_store(groups[0], (0, 1), (6, 7))
+        second_chunk_passes(2, (0, 1))
+        kind1(groups[1], 0)
+        kind1(groups[1], 1)
+        pack_sinc(2, 1)
+        turn_and_store(groups[0], (2, 3), (6, 7))
+        kind1(groups[1], 2)
+        quantize_sinc(2, 1)
+        kind1(groups[1], 3)
+        second_chunk_passes(2, (2, 3))
+        pack_h(1, 1)
+        pack_h(1, 2)
+        quantize_h(1, 1)
+        quantize_h(1, 2)
+        kind0(groups[2], 0)
+        kind0(groups[2], 1)
+        second_chunk_passes(3, (0, 1))
+        kind0(groups[2], 2)
+        kind0(groups[2], 3)
+        second_chunk_passes(3, (2, 3))
+        turn_and_store(groups[1], (0, 1), (6, 7))
+        kind1(groups[2], 0)
+        kind1(groups[2], 1)
+        pack_h(1, 3)
+        turn_and_store(groups[1], (2, 3), (4, 5))
+        kind1(groups[2], 2)
+        quantize_h(1, 3)
+        kind1(groups[2], 3)
+        waiting = [(0, 1), (2, 3), (4,), (5,)]
+        for n in range(CG, len(groups)):
+            grp, before = groups[n], groups[n - 1]
+            ready = [groups[k] for k in waiting[n - CG]]
+            for done in ready:
+                pack_y(done)
+            for done in ready:
+                quantize_y(done)
+            if n in (4, 5):
+                store_y_scales(n - 4, n - 3)
+            kind0_all(grp)
+            blocks = range(before[1] // P)
+            turn_and_store(before, blocks, [4 + b for b in blocks])
+            kind1_all(grp)
+        last = groups[-1]
+        pack_y(last)
+        turn_and_store(last, (0, 1), (6, 7))
+        quantize_y(last)
+        store_y_scales(2, 3)

@@ -37,7 +37,7 @@ def tile_powder_pattern_sinc_k5_kernel(
         psum = ctx.enter_context(tc.psum_pool(name="psum", bufs=1))
         ctx.enter_context(tc.manual_schedule())
 
-        def bank(n):
+        def bank():
             return psum.tile([P, W], F32, name="bank", bufs=8)
 
         c_words = keep.tile([P, 2 * S], U8, align_bytes=64)
@@ -55,7 +55,7 @@ def tile_powder_pattern_sinc_k5_kernel(
         d_vec_in = keep.tile([P, W], BF16, align_bytes=64)
         c_vec_in = keep.tile([P, W], BF16, align_bytes=64)
         d_rows = keep.tile([P, T, P], F32, align_bytes=64)
-        c_rows = keep.tile([P, T, P], F32, align_bytes=64)
+        ident_bf16 = keep.tile([P, P], BF16, align_bytes=64)
         d_vec = keep.tile([P, T, D_ROWS], F32, align_bytes=64)
         c_vec = keep.tile([P, T, C_ROWS], F32, align_bytes=64)
         ident = keep.tile([P, P], F32, align_bytes=64)
@@ -63,10 +63,11 @@ def tile_powder_pattern_sinc_k5_kernel(
         nc.vector.memset(d_scales_in[:].bitcast(I32), 0)
         nc.vector.memset(c_scales[:].bitcast(I32), 0)
         nc.vector.memset(d_rows[:], 0.0)
+        nc.vector.memset(c_vec_in[:], 0.0)
         make_identity(nc, ident[:])
+        nc.scalar.activation(out=ident_bf16[:], in_=ident[:], func=IDENT)
         nc.gpsimd.dma_start(out=c_vec_in[ROW_FORM:ROW_SELF, :], in_=form.rearrange("a (g n) -> (a g) n", n=W))
         nc.gpsimd.dma_start(out=c_vec_in[ROW_SELF:C_ROWS, :], in_=selfscat.rearrange("(g n) -> g n", n=W))
-        nc.vector.memset(c_rows[:], 0.0)
 
         def load_words(dst, src, lo, hi):
             nc.sync.dma_start(out=dst[:, lo:hi].bitcast(I32), in_=src[0, :, lo:hi].bitcast(I32))
@@ -98,20 +99,22 @@ def tile_powder_pattern_sinc_k5_kernel(
             for g in range(DG):
                 load_sinc(cg, g)
 
-        def turn_vectors(rows, vec, bank_no):
-            ps = bank(bank_no)
-            for t in range(T):
-                nc.tensor.transpose(ps[:, P * t : P * (t + 1)], rows[:, t, :], ident[:])
-            nc.scalar.activation(
-                out=vec[:], in_=ps[:].rearrange("p (t j) -> p t j", t=T)[:, :, 0 : vec.shape[2]], func=IDENT
-            )
-
-        nc.scalar.activation(
+        nc.vector.tensor_copy(
             out=d_rows[0:D_ROWS, :, :].rearrange("j t (q r) -> j t q r", r=8),
             in_=d_vec_in[0:D_ROWS, :].rearrange("j (q t r) -> j t q r", t=T, r=8),
-            func=IDENT,
         )
-        turn_vectors(d_rows, d_vec, 0)
+        d_turned = bank()
+        for t in range(T):
+            nc.tensor.transpose(d_turned[:, P * t : P * (t + 1)], d_rows[:, t, :], ident[:])
+        nc.scalar.activation(out=d_vec[:], in_=d_turned[:].rearrange("p (t j) -> p t j", t=T)[:, :, 0:D_ROWS], func=IDENT)
+
+        def turn_c_rows():
+            c_turned = psum.tile([P, W], BF16, name="bank", bufs=8)
+            for u in range(T):
+                nc.tensor.transpose(c_turned[:, P * u : P * (u + 1)], c_vec_in[:, u:W:T], ident_bf16[:])
+            nc.scalar.activation(
+                out=c_vec[:], in_=c_turned[:].rearrange("p (u j) -> p u j", u=T)[:, :, 0:C_ROWS], func=IDENT
+            )
 
         def order_modes(j):
             nc.vector.tensor_copy(
@@ -123,14 +126,21 @@ def tile_powder_pattern_sinc_k5_kernel(
                 in_=d_scales_in[:, W * j : W * (j + 1)].bitcast(I32).rearrange("p (q t w) -> p t q w", t=T, w=2),
             )
 
-        h_ps, h_rows, h_packed, sinc_packed = {}, {}, {}, {}
+        h_rows, h_packed, sinc_packed = {}, {}, {}
         part, first_term, y_rows, y_packed, turned = {}, {}, {}, {}, {}
 
-        def weights_pass(ch, j, t, bank_no):
-            h_ps[ch, j, t] = bank(bank_no)
+        def scale_and_shift(dst, src, scale_col, shift_col, on_vector):
+            if on_vector:
+                nc.vector.tensor_scalar(dst, src, scale_col, shift_col, MULT, ADD)
+            else:
+                nc.scalar.activation(out=dst, in_=src, func=IDENT, scale=scale_col, bias=shift_col)
+
+        def weights(ch, w, on_vector=False):
+            j, t = divmod(w, T)
+            acc = bank()
             col = W * j + P * t
             nc.tensor.matmul_mx(
-                out=h_ps[ch, j, t][:],
+                out=acc[:],
                 lhsT=d_words[:, 2 * col : 2 * (col + P)].bitcast(FP4X4),
                 lhsT_scale=d_scales[:, col : col + P],
                 rhs=c_words[:, 2 * W * ch : 2 * W * (ch + 1)].bitcast(FP4X4),
@@ -140,25 +150,32 @@ def tile_powder_pattern_sinc_k5_kernel(
             )
             if t == 0:
                 h_rows[ch, j] = work.tile([P, T, W], BF16, name="h_rows", align_bytes=64, bufs=4)
-
-        def correct_weights(ch, j, t, on_vector):
-            gain_col = d_vec[:, t, ROW_GAIN + j : ROW_GAIN + j + 1]
-            base_col = d_vec[:, t, ROW_BASE + j : ROW_BASE + j + 1]
-            if on_vector:
-                nc.vector.tensor_scalar(h_rows[ch, j][:, t, :], h_ps[ch, j, t][:], gain_col, base_col, MULT, ADD)
-            else:
-                nc.scalar.activation(
-                    out=h_rows[ch, j][:, t, :], in_=h_ps[ch, j, t][:], func=IDENT, scale=gain_col, bias=base_col
-                )
-
-        def interleave(dst, src):
-            nc.vector.tensor_copy(
-                out=dst.rearrange("p (c i) t -> p c t i", i=4), in_=src.rearrange("p t (c i) -> p c t i", i=4)
+            scale_and_shift(
+                h_rows[ch, j][:, t, :],
+                acc[:],
+                d_vec[:, t, ROW_GAIN + j : ROW_GAIN + j + 1],
+                d_vec[:, t, ROW_BASE + j : ROW_BASE + j + 1],
+                on_vector,
             )
 
-        def pack_h(ch, j):
-            h_packed[ch, j] = work.tile([P, W, T], BF16, name="packed", align_bytes=64, bufs=3)
-            interleave(h_packed[ch, j][:], h_rows[ch, j][:])
+        def pack(dst, src, scalar_halves):
+            half = dst.shape[1] // 2
+            if len(scalar_halves) == 0:
+                nc.vector.tensor_copy(out=dst, in_=src)
+            elif len(scalar_halves) == 2:
+                nc.scalar.copy(out=dst, in_=src)
+            else:
+                on_scalar = slice(half * scalar_halves[0], half * (scalar_halves[0] + 1))
+                on_vector = slice(half * (1 - scalar_halves[0]), half * (2 - scalar_halves[0]))
+                nc.scalar.copy(out=dst[:, on_scalar], in_=src[:, on_scalar])
+                nc.vector.tensor_copy(out=dst[:, on_vector], in_=src[:, on_vector])
+
+        def interleave(dst, src, scalar_halves):
+            pack(dst.rearrange("p (c i) t -> p c t i", i=4), src.rearrange("p t (c i) -> p c t i", i=4), scalar_halves)
+
+        def pack_h(ch, j, scalar_halves=()):
+            h_packed[ch, j] = work.tile([P, W, T], BF16, name="packed", align_bytes=64, bufs=4)
+            interleave(h_packed[ch, j][:], h_rows[ch, j][:], scalar_halves)
 
         def quantize_h(ch, j):
             nc.vector.quantize_mx(
@@ -167,11 +184,12 @@ def tile_powder_pattern_sinc_k5_kernel(
                 in_=h_packed[ch, j][:].rearrange("p i t -> p (i t)"),
             )
 
-        def pack_sinc(cg, g):
-            sinc_packed[cg, g] = work.tile([P, W, T], BF16, name="packed", align_bytes=64, bufs=3)
-            nc.vector.tensor_copy(
-                out=sinc_packed[cg, g][:].rearrange("p (u m) t -> p m t u", u=T),
-                in_=sinc_in[:, cg, g, :, :].rearrange("p t (m u) -> p m t u", u=T),
+        def pack_sinc(cg, g, scalar_halves=()):
+            sinc_packed[cg, g] = work.tile([P, W, T], BF16, name="packed", align_bytes=64, bufs=4)
+            pack(
+                sinc_packed[cg, g][:].rearrange("p (u m) t -> p m t u", u=T),
+                sinc_in[:, cg, g, :, :].rearrange("p t (m u) -> p m t u", u=T),
+                scalar_halves,
             )
 
         def quantize_sinc(cg, g):
@@ -181,13 +199,16 @@ def tile_powder_pattern_sinc_k5_kernel(
                 in_=sinc_packed[cg, g][:].rearrange("p c t -> p (c t)"),
             )
 
+        groups = [(W * ch, W, cg) for ch in range(CHUNKS) for cg in range(CG)]
+        groups = groups[:-1] + [(W, W // 2, CG - 1), (W + W // 2, W // 2, CG - 1)]
+
         def partial_pattern(grp, u, a):
-            first, n, cg = grp
+            first, n, cg = groups[grp]
             ch, lo = divmod(first, W)
-            part[grp, u, a] = bank(u)
+            acc = bank()
             for g in range(DG):
                 nc.tensor.matmul_mx(
-                    out=part[grp, u, a][:, 0:n],
+                    out=acc[:, 0:n],
                     lhsT=sinc_codes[:, cg, g, P * u : P * (u + 1)].bitcast(FP8X4),
                     lhsT_scale=sinc_scales[:, cg, g, P * u : P * (u + 1)],
                     rhs=h_codes[:, ch, DG * a + g, lo : lo + n].bitcast(FP8X4),
@@ -195,40 +216,41 @@ def tile_powder_pattern_sinc_k5_kernel(
                     start=(g == 0),
                     stop=(g == DG - 1),
                 )
+            return acc[:, 0:n]
 
-        def kind0(grp, u):
-            first, n, cg = grp
-            partial_pattern(grp, u, 0)
-            first_term[grp, u] = work.tile([P, W], F32, name="first_term", align_bytes=64, bufs=4)
-            nc.scalar.activation(
-                out=first_term[grp, u][:, 0:n],
-                in_=part[grp, u, 0][:, 0:n],
-                func=IDENT,
-                scale=c_vec[:, u, ROW_FORM + cg : ROW_FORM + cg + 1],
-                bias=c_vec[:, u, ROW_SELF + cg : ROW_SELF + cg + 1],
+        def kind0(grp, u, on_vector=False):
+            first, n, cg = groups[grp]
+            acc = partial_pattern(grp, u, 0)
+            first_term[grp, u] = work.tile([P, W], F32, name="first_term", align_bytes=64, bufs=5)
+            scale_and_shift(
+                first_term[grp, u][:, 0:n],
+                acc,
+                c_vec[:, u, ROW_FORM + cg : ROW_FORM + cg + 1],
+                c_vec[:, u, ROW_SELF + cg : ROW_SELF + cg + 1],
+                on_vector,
             )
 
         def kind1(grp, u):
-            first, n, cg = grp
-            partial_pattern(grp, u, 1)
+            first, n, cg = groups[grp]
+            acc = partial_pattern(grp, u, 1)
             if u == 0:
                 y_rows[grp] = work.tile([P, T, W], F32, name="y_rows", align_bytes=64, bufs=6)
             nc.vector.scalar_tensor_tensor(
                 out=y_rows[grp][:, u, 0:n],
-                in0=part[grp, u, 1][:, 0:n],
+                in0=acc,
                 scalar=c_vec[:, u, ROW_FORM + CG + cg : ROW_FORM + CG + cg + 1],
                 in1=first_term[grp, u][:, 0:n],
                 op0=MULT,
                 op1=ADD,
             )
 
-        def pack_y(grp):
-            first, n, cg = grp
-            y_packed[grp] = work.tile([P, W, T], BF16, name="packed", align_bytes=64, bufs=3)
-            interleave(y_packed[grp][:, 0:n, :], y_rows[grp][:, :, 0:n])
+        def pack_y(grp, scalar_halves=()):
+            first, n, cg = groups[grp]
+            y_packed[grp] = work.tile([P, W, T], BF16, name="packed", align_bytes=64, bufs=4)
+            interleave(y_packed[grp][:, 0:n, :], y_rows[grp][:, :, 0:n], scalar_halves)
 
         def quantize_y(grp):
-            first, n, cg = grp
+            first, n, cg = groups[grp]
             y_codes = work.tile([P, W], U32, name="y_codes", align_bytes=64, bufs=3)
             nc.vector.quantize_mx(
                 out=y_codes[:, 0:n].bitcast(FP8X4),
@@ -239,145 +261,162 @@ def tile_powder_pattern_sinc_k5_kernel(
                 out=out_1[cg, :, first : first + n, :].rearrange("p m t -> p (m t)").bitcast(I32),
                 in_=y_codes[:, 0:n].bitcast(I32),
             )
+            if first + n == S and cg > 0:
+                done = slice(0, CG - 1) if cg < CG - 1 else slice(CG - 1, CG)
+                for quad in range(4):
+                    nc.sync.dma_start(
+                        out=out_2[done, 4 * quad : 4 * quad + 4, :].rearrange("g r m -> r g m").bitcast(I32),
+                        in_=y_scales[32 * quad : 32 * quad + 4, done, :].bitcast(I32),
+                    )
 
-        def store_y_scales(cg_lo, cg_hi):
-            for quad in range(4):
-                nc.sync.dma_start(
-                    out=out_2[cg_lo:cg_hi, 4 * quad : 4 * quad + 4, :].rearrange("g r m -> r g m").bitcast(I32),
-                    in_=y_scales[32 * quad : 32 * quad + 4, cg_lo:cg_hi, :].bitcast(I32),
-                )
-
-        def turn_y(grp, blocks, banks, slots):
-            for b, bank_no in zip(blocks, banks):
-                if slots[0] == 0:
-                    turned[grp, b] = bank(bank_no)
-                for u in slots:
+        def turn_y(grp, blocks):
+            for b in blocks:
+                turned[grp, b] = bank()
+                for u in range(T):
                     nc.tensor.transpose(
                         turned[grp, b][:, P * u : P * (u + 1)], y_rows[grp][:, u, P * b : P * (b + 1)], ident[:]
                     )
 
-        def store_y(grp, b, on_vector=False):
-            first, n, cg = grp
-            y_out = work.tile([P, W], F32, name="y_out", align_bytes=64, bufs=6)
-            dst = y_out[:].rearrange("i (m u) -> i m u", u=T)
-            src = turned[grp, b][:].rearrange("i (u m) -> i m u", u=T)
-            if on_vector:
-                nc.vector.tensor_copy(out=dst, in_=src)
-            else:
-                nc.scalar.copy(out=dst, in_=src)
-            nc.sync.dma_start(out=out_0[first + P * b : first + P * (b + 1), W * cg : W * (cg + 1)], in_=y_out[:])
+        def store_y(grp, blocks, on_vector=()):
+            first, n, cg = groups[grp]
+            for b in blocks:
+                y_out = work.tile([P, W], F32, name="y_out", align_bytes=64, bufs=8)
+                dst = y_out[:].rearrange("i (m u) -> i m u", u=T)
+                src = turned[grp, b][:].rearrange("i (u m) -> i m u", u=T)
+                if b in on_vector:
+                    nc.vector.tensor_copy(out=dst, in_=src)
+                else:
+                    nc.scalar.copy(out=dst, in_=src)
+                nc.sync.dma_start(out=out_0[first + P * b : first + P * (b + 1), W * cg : W * (cg + 1)], in_=y_out[:])
 
-        groups = [(W * ch, W, cg) for ch in range(CHUNKS) for cg in range(CG)]
-        groups = groups[:-1] + [(W, W // 2, CG - 1), (W + W // 2, W // 2, CG - 1)]
-        ALL = (0, 1, 2, 3)
+        def emit_y(grp, blocks, on_vector=()):
+            turn_y(grp, blocks)
+            store_y(grp, blocks, on_vector)
 
         order_modes(0)
         order_modes(1)
         pack_sinc(0, 0)
         order_modes(2)
         order_modes(3)
-        for j in range(KINDS * DG):
-            for t in range(T):
-                weights_pass(0, j, t, 4 + t)
-                correct_weights(0, j, t, False)
-            if j == 0:
-                nc.scalar.activation(
-                    out=c_rows[0:C_ROWS, :, :], in_=c_vec_in[0:C_ROWS, :].rearrange("j (m t) -> j t m", t=T), func=IDENT
-                )
-            if j == 1:
-                turn_vectors(c_rows, c_vec, 1)
-        quantize_sinc(0, 0)
         pack_sinc(0, 1)
+        quantize_sinc(0, 0)
+        for w in range(0, 8):
+            weights(0, w)
         pack_h(0, 0)
         quantize_sinc(0, 1)
         quantize_h(0, 0)
         pack_h(0, 1)
+        for w in range(8, 13):
+            weights(0, w, w == 10)
+        turn_c_rows()
         quantize_h(0, 1)
+        for w in range(13, 16):
+            weights(0, w, w == 13)
         pack_h(0, 2)
-        for u in range(T):
-            kind0(groups[0], u)
+        weights(1, 0)
+        pack_h(0, 3, (1,))
         quantize_h(0, 2)
-        pack_h(0, 3)
         quantize_h(0, 3)
         pack_sinc(1, 0)
-
-        def second_chunk_passes(j, slots):
-            for t in slots:
-                weights_pass(1, j, t, 4 + t % 2)
-                correct_weights(1, j, t, False)
-
-        def kind0_all(grp):
-            for u in range(T):
-                kind0(grp, u)
-
-        def kind1_all(grp):
-            for u in range(T):
-                kind1(grp, u)
-
-        def turn_and_store(grp, blocks, banks):
-            turn_y(grp, blocks, banks, ALL)
-            for b in blocks:
-                store_y(grp, b)
-
-        second_chunk_passes(0, (0, 1))
-        kind1(groups[0], 0)
-        quantize_sinc(1, 0)
-        kind1(groups[0], 1)
-        second_chunk_passes(0, (2, 3))
         pack_sinc(1, 1)
-        kind1(groups[0], 2)
+        quantize_sinc(1, 0)
+        weights(1, 1)
+        weights(1, 2)
+        kind0(0, 0)
+        weights(1, 3)
+        kind0(0, 1)
+        kind0(0, 2)
+        weights(1, 4)
+        kind1(0, 0)
         quantize_sinc(1, 1)
-        kind1(groups[0], 3)
-        second_chunk_passes(1, ALL)
+        kind0(0, 3)
+        weights(1, 5)
+        kind1(0, 1)
+        kind1(0, 2)
+        for w in range(6, 9):
+            weights(1, w)
         pack_sinc(2, 0)
-        pack_h(1, 0)
+        pack_sinc(2, 1, (1,))
+        kind1(0, 3)
+        kind0(1, 0)
+        kind1(1, 0)
         quantize_sinc(2, 0)
-        quantize_h(1, 0)
-        kind0_all(groups[1])
-        turn_and_store(groups[0], (0, 1), (6, 7))
-        second_chunk_passes(2, (0, 1))
-        kind1(groups[1], 0)
-        kind1(groups[1], 1)
-        pack_sinc(2, 1)
-        turn_and_store(groups[0], (2, 3), (6, 7))
-        kind1(groups[1], 2)
         quantize_sinc(2, 1)
-        kind1(groups[1], 3)
-        second_chunk_passes(2, (2, 3))
+        weights(1, 9)
+        for u in (1, 2):
+            kind0(1, u)
+            kind1(1, u)
+        for w in range(10, 13):
+            weights(1, w)
+        pack_h(1, 0)
+        kind0(1, 3)
+        kind1(1, 3)
+        weights(1, 13)
+        weights(1, 14)
         pack_h(1, 1)
         pack_h(1, 2)
+        quantize_h(1, 0)
         quantize_h(1, 1)
+        emit_y(0, range(4))
+        weights(1, 15)
+        kind0(2, 0)
+        kind1(2, 0)
         quantize_h(1, 2)
-        kind0(groups[2], 0)
-        kind0(groups[2], 1)
-        second_chunk_passes(3, (0, 1))
-        kind0(groups[2], 2)
-        kind0(groups[2], 3)
-        second_chunk_passes(3, (2, 3))
-        turn_and_store(groups[1], (0, 1), (6, 7))
-        kind1(groups[2], 0)
-        kind1(groups[2], 1)
-        pack_h(1, 3)
-        turn_and_store(groups[1], (2, 3), (4, 5))
-        kind1(groups[2], 2)
+        kind0(2, 1)
+        kind1(2, 1)
+        pack_h(1, 3, (0, 1))
+        kind0(2, 2, True)
+        kind0(2, 3, True)
+        emit_y(1, range(4))
+        kind0(3, 0, True)
         quantize_h(1, 3)
-        kind1(groups[2], 3)
-        waiting = [(0, 1), (2, 3), (4,), (5,)]
-        for n in range(CG, len(groups)):
-            grp, before = groups[n], groups[n - 1]
-            ready = [groups[k] for k in waiting[n - CG]]
-            for done in ready:
-                pack_y(done)
-            for done in ready:
-                quantize_y(done)
-            if n in (4, 5):
-                store_y_scales(n - 4, n - 3)
-            kind0_all(grp)
-            blocks = range(before[1] // P)
-            turn_and_store(before, blocks, [4 + b for b in blocks])
-            kind1_all(grp)
-        last = groups[-1]
-        pack_y(last)
-        turn_and_store(last, (0, 1), (6, 7))
-        quantize_y(last)
-        store_y_scales(2, 3)
+        pack_y(0, (1,))
+        kind1(2, 2)
+        kind1(2, 3)
+        kind0(3, 1)
+        kind0(3, 2)
+        kind1(3, 0)
+        kind0(3, 3, True)
+        pack_y(1, (0,))
+        for u in range(1, 4):
+            kind1(3, u)
+        emit_y(2, range(4), (1,))
+        pack_y(2)
+        for u in range(3):
+            quantize_y(u)
+            kind0(4, u)
+            if u == 2:
+                pack_y(3, (0,))
+            kind1(4, u)
+        kind0(4, 3)
+        kind1(4, 3)
+        emit_y(3, range(4))
+        quantize_y(3)
+        pack_y(4)
+        for u in range(3):
+            kind0(5, u)
+        kind1(5, 0)
+        quantize_y(4)
+        kind0(5, 3)
+        kind1(5, 1)
+        kind0(6, 0)
+        kind0(6, 1)
+        kind1(5, 2)
+        kind1(5, 3)
+        turn_y(4, range(4))
+        store_y(4, range(3))
+        pack_y(5)
+        quantize_y(5)
+        turn_y(5, (0,))
+        kind0(6, 2)
+        kind1(6, 0)
+        kind0(6, 3, True)
+        kind1(6, 1)
+        kind1(6, 2)
+        store_y(4, (3,))
+        store_y(5, (0,))
+        kind1(6, 3)
+        emit_y(5, (1,), (1,))
+        pack_y(6)
+        emit_y(6, range(2))
+        quantize_y(6)

@@ -3,8 +3,8 @@ from contextlib import ExitStack
 import concourse.mybir as mybir
 from concourse.masks import make_identity
 
-S, KINDS, MODES, R, Q = 1024, 2, 512, 1024, 1536
-FLOPS = 2 * S * MODES * KINDS * R + 2 * S * KINDS * R * Q
+SAMPLES, KINDS, MODES, DISTANCES, VECTORS = 1024, 2, 512, 1024, 1536
+FLOPS = 2 * SAMPLES * MODES * KINDS * DISTANCES + 2 * SAMPLES * KINDS * DISTANCES * VECTORS
 
 F32 = mybir.dt.float32
 BF16 = mybir.dt.bfloat16
@@ -13,18 +13,33 @@ U32 = mybir.dt.uint32
 U8 = mybir.dt.uint8
 FP8X4 = mybir.dt.float8_e4m3fn_x4
 FP4X4 = mybir.dt.float4_e2m1fn_x4
-IDENT = mybir.ActivationFunctionType.Identity
+IDENTITY = mybir.ActivationFunctionType.Identity
 MULT = mybir.AluOpType.mult
 ADD = mybir.AluOpType.add
 
 P = 128
-T = 4
-W = 512
-CHUNKS = S // W
-DG = R // W
-CG = Q // W
-ROW_GAIN, ROW_BASE, D_ROWS = 0, 4, 8
-ROW_FORM, ROW_SELF, C_ROWS = 0, 6, 9
+SLOTS = 4
+RUN = 8
+W = P * SLOTS
+QUADRANTS = 4
+ALIGN = 64
+CHUNKS = SAMPLES // W
+D_PASSES = DISTANCES // W
+H_TILES = KINDS * D_PASSES
+C_GROUPS = VECTORS // W
+
+ROW_GAIN, ROW_BASE, D_ROWS = 0, H_TILES, 2 * H_TILES
+ROW_FORM, ROW_SELF, C_ROWS = 0, KINDS * C_GROUPS, (KINDS + 1) * C_GROUPS
+
+GROUPS = [(W * ch, W, cg) for ch in range(CHUNKS) for cg in range(C_GROUPS)][:-1] + [
+    (SAMPLES - W, W // 2, C_GROUPS - 1),
+    (SAMPLES - W // 2, W // 2, C_GROUPS - 1),
+]
+
+BANKS = 8
+H_ROWS_BUFS, PACKED_BUFS, FIRST_TERM_BUFS, Y_ROWS_BUFS, Y_CODES_BUFS, Y_OUT_BUFS = 4, 4, 5, 6, 3, 8
+
+FIRST_HALF, SECOND_HALF = 0, 1
 
 
 def tile_powder_pattern_sinc_k5_kernel(
@@ -33,390 +48,386 @@ def tile_powder_pattern_sinc_k5_kernel(
     nc = tc.nc
     with ExitStack() as ctx:
         keep = ctx.enter_context(tc.tile_pool(name="keep", bufs=1))
-        work = ctx.enter_context(tc.tile_pool(name="work", bufs=2))
-        psum = ctx.enter_context(tc.psum_pool(name="psum", bufs=1))
+        work = ctx.enter_context(tc.tile_pool(name="work", bufs=1))
+        psum = ctx.enter_context(tc.psum_pool(name="psum", bufs=BANKS))
         ctx.enter_context(tc.manual_schedule())
 
-        def bank():
-            return psum.tile([P, W], F32, name="bank", bufs=8)
+        def next_bank(dtype):
+            return psum.tile([P, W], dtype, name="bank")
 
-        c_words = keep.tile([P, 2 * S], U8, align_bytes=64)
-        c_scales = keep.tile([P, S], U8, align_bytes=64)
-        d_words_in = keep.tile([P, 2 * KINDS * R], U8, align_bytes=64)
-        d_scales_in = keep.tile([P, KINDS * R], U8, align_bytes=64)
-        d_words = keep.tile([P, 2 * KINDS * R], U8, align_bytes=64)
-        d_scales = keep.tile([P, KINDS * R], U8, align_bytes=64)
-        sinc_in = keep.tile([P, CG, DG, T, W], BF16, align_bytes=64)
-        sinc_codes = keep.tile([P, CG, DG, W], U32, align_bytes=64)
-        sinc_scales = keep.tile([P, CG, DG, W], U8, align_bytes=64)
-        h_codes = keep.tile([P, CHUNKS, KINDS * DG, W], U32, align_bytes=64)
-        h_scales = keep.tile([P, CHUNKS, KINDS * DG, W], U8, align_bytes=64)
-        y_scales = keep.tile([P, CG, S], U8, align_bytes=64)
-        d_vec_in = keep.tile([P, W], BF16, align_bytes=64)
-        c_vec_in = keep.tile([P, W], BF16, align_bytes=64)
-        d_rows = keep.tile([P, T, P], F32, align_bytes=64)
-        ident_bf16 = keep.tile([P, P], BF16, align_bytes=64)
-        d_vec = keep.tile([P, T, D_ROWS], F32, align_bytes=64)
-        c_vec = keep.tile([P, T, C_ROWS], F32, align_bytes=64)
-        ident = keep.tile([P, P], F32, align_bytes=64)
+        coef_sb = keep.tile([P, 2 * SAMPLES], U8, align_bytes=ALIGN)
+        modes_in = keep.tile([P, 2 * KINDS * DISTANCES], U8, align_bytes=ALIGN)
+        modes_sb = keep.tile([P, 2 * KINDS * DISTANCES], U8, align_bytes=ALIGN)
+        coef_scales_sb = keep.tile([P, SAMPLES], U8, align_bytes=ALIGN)
+        modes_scales_in = keep.tile([P, KINDS * DISTANCES], U8, align_bytes=ALIGN)
+        modes_scales_sb = keep.tile([P, KINDS * DISTANCES], U8, align_bytes=ALIGN)
+        sinc_rows = keep.tile([P, C_GROUPS, D_PASSES, SLOTS, W], BF16, align_bytes=ALIGN)
+        sinc_codes = keep.tile([P, C_GROUPS, D_PASSES, W], U32, align_bytes=ALIGN)
+        sinc_scales = keep.tile([P, C_GROUPS, D_PASSES, W], U8, align_bytes=ALIGN)
+        h_codes = keep.tile([P, CHUNKS, H_TILES, W], U32, align_bytes=ALIGN)
+        h_scales = keep.tile([P, CHUNKS, H_TILES, W], U8, align_bytes=ALIGN)
+        y_scales = keep.tile([P, C_GROUPS, SAMPLES], U8, align_bytes=ALIGN)
+        d_vec_in = keep.tile([P, W], BF16, align_bytes=ALIGN)
+        d_vec_rows = keep.tile([P, SLOTS, P], F32, align_bytes=ALIGN)
+        d_vec = keep.tile([P, SLOTS, D_ROWS], F32, align_bytes=ALIGN)
+        c_vec_in = keep.tile([P, W], BF16, align_bytes=ALIGN)
+        c_vec = keep.tile([P, SLOTS, C_ROWS], F32, align_bytes=ALIGN)
+        ident = keep.tile([P, P], F32, align_bytes=ALIGN)
+        ident_bf16 = keep.tile([P, P], BF16, align_bytes=ALIGN)
 
-        nc.vector.memset(d_scales_in[:].bitcast(I32), 0)
-        nc.vector.memset(c_scales[:].bitcast(I32), 0)
-        nc.vector.memset(d_rows[:], 0.0)
+        nc.vector.memset(modes_scales_in[:].bitcast(I32), 0)
+        nc.vector.memset(coef_scales_sb[:].bitcast(I32), 0)
+        nc.vector.memset(d_vec_rows[:], 0.0)
         nc.vector.memset(c_vec_in[:], 0.0)
         make_identity(nc, ident[:])
-        nc.scalar.activation(out=ident_bf16[:], in_=ident[:], func=IDENT)
+        nc.scalar.activation(out=ident_bf16[:], in_=ident[:], func=IDENTITY)
         nc.gpsimd.dma_start(out=c_vec_in[ROW_FORM:ROW_SELF, :], in_=form.rearrange("a (g n) -> (a g) n", n=W))
         nc.gpsimd.dma_start(out=c_vec_in[ROW_SELF:C_ROWS, :], in_=selfscat.rearrange("(g n) -> g n", n=W))
 
-        def load_words(dst, src, lo, hi):
-            nc.sync.dma_start(out=dst[:, lo:hi].bitcast(I32), in_=src[0, :, lo:hi].bitcast(I32))
+        def load_words(dst, src, first_column, columns):
+            span = slice(2 * first_column, 2 * (first_column + columns))
+            nc.sync.dma_start(out=dst[:, span].bitcast(I32), in_=src[0, :, span].bitcast(I32))
+
+        def load_scales(dst, src):
+            for quad in range(QUADRANTS):
+                nc.sync.dma_start(
+                    out=dst[32 * quad : 32 * quad + 4, :].bitcast(I32), in_=src[0, 4 * quad : 4 * quad + 4, :].bitcast(I32)
+                )
 
         def load_sinc(cg, g):
-            rows = sinc[W * g : W * (g + 1), W * cg : W * (cg + 1)].rearrange("(q t r) c -> t q r c", t=T, r=8)
-            for t in range(T):
-                nc.sync.dma_start(out=sinc_in[:, cg, g, t, :], in_=rows[t])
+            rows = sinc[W * g : W * (g + 1), W * cg : W * (cg + 1)].rearrange("(q t r) c -> t q r c", t=SLOTS, r=RUN)
+            for t in range(SLOTS):
+                nc.sync.dma_start(out=sinc_rows[:, cg, g, t, :], in_=rows[t])
 
-        load_words(d_words_in, modes_words, 0, 2 * R)
-        load_words(c_words, coef_words, 0, 2 * W)
+        load_words(modes_in, modes_words, 0, DISTANCES)
+        load_words(coef_sb, coef_words, 0, W)
         nc.sync.dma_start(out=d_vec_in[ROW_GAIN:ROW_BASE, :], in_=gain.rearrange("(j n) -> j n", n=W))
         nc.sync.dma_start(out=d_vec_in[ROW_BASE:D_ROWS, :], in_=base.rearrange("(j n) -> j n", n=W))
-        for quad in range(4):
-            nc.sync.dma_start(
-                out=d_scales_in[32 * quad : 32 * quad + 4, :].bitcast(I32),
-                in_=modes_scales[0, 4 * quad : 4 * quad + 4, :].bitcast(I32),
-            )
-        for quad in range(4):
-            nc.sync.dma_start(
-                out=c_scales[32 * quad : 32 * quad + 4, :].bitcast(I32),
-                in_=coef_scales[0, 4 * quad : 4 * quad + 4, :].bitcast(I32),
-            )
+        load_scales(modes_scales_in, modes_scales)
+        load_scales(coef_scales_sb, coef_scales)
         load_sinc(0, 0)
-        load_words(d_words_in, modes_words, 2 * R, 4 * R)
+        load_words(modes_in, modes_words, DISTANCES, DISTANCES)
         load_sinc(0, 1)
-        load_words(c_words, coef_words, 2 * W, 4 * W)
-        for cg in range(1, CG):
-            for g in range(DG):
+        load_words(coef_sb, coef_words, W, W)
+        for cg in range(1, C_GROUPS):
+            for g in range(D_PASSES):
                 load_sinc(cg, g)
 
         nc.vector.tensor_copy(
-            out=d_rows[0:D_ROWS, :, :].rearrange("j t (q r) -> j t q r", r=8),
-            in_=d_vec_in[0:D_ROWS, :].rearrange("j (q t r) -> j t q r", t=T, r=8),
+            out=d_vec_rows[0:D_ROWS, :, :].rearrange("j t (q r) -> j t q r", r=RUN),
+            in_=d_vec_in[0:D_ROWS, :].rearrange("j (q t r) -> j t q r", t=SLOTS, r=RUN),
         )
-        d_turned = bank()
-        for t in range(T):
-            nc.tensor.transpose(d_turned[:, P * t : P * (t + 1)], d_rows[:, t, :], ident[:])
-        nc.scalar.activation(out=d_vec[:], in_=d_turned[:].rearrange("p (t j) -> p t j", t=T)[:, :, 0:D_ROWS], func=IDENT)
+        d_turned = next_bank(F32)
+        for t in range(SLOTS):
+            nc.tensor.transpose(d_turned[:, P * t : P * (t + 1)], d_vec_rows[:, t, :], ident[:])
+        nc.scalar.activation(
+            out=d_vec[:], in_=d_turned[:].rearrange("p (t j) -> p t j", t=SLOTS)[:, :, 0:D_ROWS], func=IDENTITY
+        )
 
-        def turn_c_rows():
-            c_turned = psum.tile([P, W], BF16, name="bank", bufs=8)
-            for u in range(T):
-                nc.tensor.transpose(c_turned[:, P * u : P * (u + 1)], c_vec_in[:, u:W:T], ident_bf16[:])
+        def turn_c_vec():
+            c_turned = next_bank(BF16)
+            for u in range(SLOTS):
+                nc.tensor.transpose(c_turned[:, P * u : P * (u + 1)], c_vec_in[:, u:W:SLOTS], ident_bf16[:])
             nc.scalar.activation(
-                out=c_vec[:], in_=c_turned[:].rearrange("p (u j) -> p u j", u=T)[:, :, 0:C_ROWS], func=IDENT
+                out=c_vec[:], in_=c_turned[:].rearrange("p (u j) -> p u j", u=SLOTS)[:, :, 0:C_ROWS], func=IDENTITY
             )
 
-        def order_modes(j):
+        def regroup(dst, src, kind, column_bytes):
+            span = slice(column_bytes * DISTANCES * kind, column_bytes * DISTANCES * (kind + 1))
+            run_words = RUN * column_bytes // 4
             nc.vector.tensor_copy(
-                out=d_words[:, 2 * W * j : 2 * W * (j + 1)].bitcast(I32).rearrange("p (t q w) -> p t q w", t=T, w=4),
-                in_=d_words_in[:, 2 * W * j : 2 * W * (j + 1)].bitcast(I32).rearrange("p (q t w) -> p t q w", t=T, w=4),
-            )
-            nc.vector.tensor_copy(
-                out=d_scales[:, W * j : W * (j + 1)].bitcast(I32).rearrange("p (t q w) -> p t q w", t=T, w=2),
-                in_=d_scales_in[:, W * j : W * (j + 1)].bitcast(I32).rearrange("p (q t w) -> p t q w", t=T, w=2),
+                out=dst[:, span].bitcast(I32).rearrange("p (t b w) -> p t b w", t=SLOTS, w=run_words),
+                in_=src[:, span].bitcast(I32).rearrange("p (b t w) -> p t b w", t=SLOTS, w=run_words),
             )
 
         h_rows, h_packed, sinc_packed = {}, {}, {}
-        part, first_term, y_rows, y_packed, turned = {}, {}, {}, {}, {}
+        first_term, y_rows, y_packed = {}, {}, {}
 
         def scale_and_shift(dst, src, scale_col, shift_col, on_vector):
             if on_vector:
                 nc.vector.tensor_scalar(dst, src, scale_col, shift_col, MULT, ADD)
             else:
-                nc.scalar.activation(out=dst, in_=src, func=IDENT, scale=scale_col, bias=shift_col)
+                nc.scalar.activation(out=dst, in_=src, func=IDENTITY, scale=scale_col, bias=shift_col)
 
-        def weights(ch, w, on_vector=False):
-            j, t = divmod(w, T)
-            acc = bank()
-            col = W * j + P * t
+        def pair_weights(ch, step, on_vector=False):
+            j, t = divmod(step, SLOTS)
+            acc = next_bank(F32)
+            kind, g = divmod(j, D_PASSES)
+            col = DISTANCES * kind + DISTANCES // SLOTS * t + P * g
             nc.tensor.matmul_mx(
                 out=acc[:],
-                lhsT=d_words[:, 2 * col : 2 * (col + P)].bitcast(FP4X4),
-                lhsT_scale=d_scales[:, col : col + P],
-                rhs=c_words[:, 2 * W * ch : 2 * W * (ch + 1)].bitcast(FP4X4),
-                rhs_scale=c_scales[:, W * ch : W * (ch + 1)],
+                lhsT=modes_sb[:, 2 * col : 2 * (col + P)].bitcast(FP4X4),
+                lhsT_scale=modes_scales_sb[:, col : col + P],
+                rhs=coef_sb[:, 2 * W * ch : 2 * W * (ch + 1)].bitcast(FP4X4),
+                rhs_scale=coef_scales_sb[:, W * ch : W * (ch + 1)],
                 start=True,
                 stop=True,
             )
             if t == 0:
-                h_rows[ch, j] = work.tile([P, T, W], BF16, name="h_rows", align_bytes=64, bufs=4)
-            scale_and_shift(
-                h_rows[ch, j][:, t, :],
-                acc[:],
-                d_vec[:, t, ROW_GAIN + j : ROW_GAIN + j + 1],
-                d_vec[:, t, ROW_BASE + j : ROW_BASE + j + 1],
-                on_vector,
+                h_rows[ch, j] = work.tile([P, SLOTS, W], BF16, name="h_rows", align_bytes=ALIGN, bufs=H_ROWS_BUFS)
+            gain_col = d_vec[:, t, ROW_GAIN + j : ROW_GAIN + j + 1]
+            base_col = d_vec[:, t, ROW_BASE + j : ROW_BASE + j + 1]
+            scale_and_shift(h_rows[ch, j][:, t, :], acc[:], gain_col, base_col, on_vector)
+
+        def new_packed():
+            return work.tile([P, W, SLOTS], BF16, name="packed", align_bytes=ALIGN, bufs=PACKED_BUFS)
+
+        def pack(dst, src, walk, scalar_half):
+            if scalar_half is None:
+                nc.vector.tensor_copy(out=dst.rearrange(walk), in_=src.rearrange(walk))
+                return
+            half = dst.shape[1] // 2
+            for k in range(2):
+                span = slice(half * k, half * (k + 1))
+                if k == scalar_half:
+                    nc.scalar.copy(out=dst[:, span].rearrange(walk), in_=src[:, span].rearrange(walk))
+                else:
+                    nc.vector.tensor_copy(out=dst[:, span].rearrange(walk), in_=src[:, span].rearrange(walk))
+
+        def pack_rows(packed, rows, scalar_half):
+            pack(
+                packed.rearrange("p (c i) t -> p c i t", i=4),
+                rows.rearrange("p t (c i) -> p c i t", i=4),
+                "p c i t -> p c t i",
+                scalar_half,
             )
 
-        def pack(dst, src, scalar_halves):
-            half = dst.shape[1] // 2
-            if len(scalar_halves) == 0:
-                nc.vector.tensor_copy(out=dst, in_=src)
-            elif len(scalar_halves) == 2:
-                nc.scalar.copy(out=dst, in_=src)
-            else:
-                on_scalar = slice(half * scalar_halves[0], half * (scalar_halves[0] + 1))
-                on_vector = slice(half * (1 - scalar_halves[0]), half * (2 - scalar_halves[0]))
-                nc.scalar.copy(out=dst[:, on_scalar], in_=src[:, on_scalar])
-                nc.vector.tensor_copy(out=dst[:, on_vector], in_=src[:, on_vector])
+        def quantize(codes, scales, packed):
+            nc.vector.quantize_mx(out=codes.bitcast(FP8X4), scales=scales, in_=packed.rearrange("p i t -> p (i t)"))
 
-        def interleave(dst, src, scalar_halves):
-            pack(dst.rearrange("p (c i) t -> p c t i", i=4), src.rearrange("p t (c i) -> p c t i", i=4), scalar_halves)
-
-        def pack_h(ch, j, scalar_halves=()):
-            h_packed[ch, j] = work.tile([P, W, T], BF16, name="packed", align_bytes=64, bufs=4)
-            interleave(h_packed[ch, j][:], h_rows[ch, j][:], scalar_halves)
+        def pack_h(ch, j, scalar_half=None):
+            h_packed[ch, j] = new_packed()
+            pack_rows(h_packed[ch, j][:], h_rows[ch, j][:], scalar_half)
 
         def quantize_h(ch, j):
-            nc.vector.quantize_mx(
-                out=h_codes[:, ch, j, :].bitcast(FP8X4),
-                scales=h_scales[:, ch, j, :],
-                in_=h_packed[ch, j][:].rearrange("p i t -> p (i t)"),
-            )
+            quantize(h_codes[:, ch, j, :], h_scales[:, ch, j, :], h_packed[ch, j][:])
 
-        def pack_sinc(cg, g, scalar_halves=()):
-            sinc_packed[cg, g] = work.tile([P, W, T], BF16, name="packed", align_bytes=64, bufs=4)
+        def pack_sinc(cg, g, scalar_half=None):
+            sinc_packed[cg, g] = new_packed()
             pack(
-                sinc_packed[cg, g][:].rearrange("p (u m) t -> p m t u", u=T),
-                sinc_in[:, cg, g, :, :].rearrange("p t (m u) -> p m t u", u=T),
-                scalar_halves,
+                sinc_packed[cg, g][:].rearrange("p (u m) t -> p u m t", u=SLOTS),
+                sinc_rows[:, cg, g, :, :].rearrange("p t (m u) -> p u m t", u=SLOTS),
+                "p u m t -> p m t u",
+                scalar_half,
             )
 
         def quantize_sinc(cg, g):
-            nc.vector.quantize_mx(
-                out=sinc_codes[:, cg, g, :].bitcast(FP8X4),
-                scales=sinc_scales[:, cg, g, :],
-                in_=sinc_packed[cg, g][:].rearrange("p c t -> p (c t)"),
-            )
+            quantize(sinc_codes[:, cg, g, :], sinc_scales[:, cg, g, :], sinc_packed[cg, g][:])
 
-        groups = [(W * ch, W, cg) for ch in range(CHUNKS) for cg in range(CG)]
-        groups = groups[:-1] + [(W, W // 2, CG - 1), (W + W // 2, W // 2, CG - 1)]
-
-        def partial_pattern(grp, u, a):
-            first, n, cg = groups[grp]
+        def partial_pattern(grp, u, kind):
+            first, n, cg = GROUPS[grp]
             ch, lo = divmod(first, W)
-            acc = bank()
-            for g in range(DG):
+            acc = next_bank(F32)
+            for g in range(D_PASSES):
                 nc.tensor.matmul_mx(
                     out=acc[:, 0:n],
                     lhsT=sinc_codes[:, cg, g, P * u : P * (u + 1)].bitcast(FP8X4),
                     lhsT_scale=sinc_scales[:, cg, g, P * u : P * (u + 1)],
-                    rhs=h_codes[:, ch, DG * a + g, lo : lo + n].bitcast(FP8X4),
-                    rhs_scale=h_scales[:, ch, DG * a + g, lo : lo + n],
+                    rhs=h_codes[:, ch, D_PASSES * kind + g, lo : lo + n].bitcast(FP8X4),
+                    rhs_scale=h_scales[:, ch, D_PASSES * kind + g, lo : lo + n],
                     start=(g == 0),
-                    stop=(g == DG - 1),
+                    stop=(g == D_PASSES - 1),
                 )
             return acc[:, 0:n]
 
         def kind0(grp, u, on_vector=False):
-            first, n, cg = groups[grp]
+            n, cg = GROUPS[grp][1:]
             acc = partial_pattern(grp, u, 0)
-            first_term[grp, u] = work.tile([P, W], F32, name="first_term", align_bytes=64, bufs=5)
-            scale_and_shift(
-                first_term[grp, u][:, 0:n],
-                acc,
-                c_vec[:, u, ROW_FORM + cg : ROW_FORM + cg + 1],
-                c_vec[:, u, ROW_SELF + cg : ROW_SELF + cg + 1],
-                on_vector,
-            )
+            first_term[grp, u] = work.tile([P, W], F32, name="first_term", align_bytes=ALIGN, bufs=FIRST_TERM_BUFS)
+            form_col = c_vec[:, u, ROW_FORM + cg : ROW_FORM + cg + 1]
+            self_col = c_vec[:, u, ROW_SELF + cg : ROW_SELF + cg + 1]
+            scale_and_shift(first_term[grp, u][:, 0:n], acc, form_col, self_col, on_vector)
 
         def kind1(grp, u):
-            first, n, cg = groups[grp]
+            n, cg = GROUPS[grp][1:]
             acc = partial_pattern(grp, u, 1)
             if u == 0:
-                y_rows[grp] = work.tile([P, T, W], F32, name="y_rows", align_bytes=64, bufs=6)
+                y_rows[grp] = work.tile([P, SLOTS, W], F32, name="y_rows", align_bytes=ALIGN, bufs=Y_ROWS_BUFS)
             nc.vector.scalar_tensor_tensor(
                 out=y_rows[grp][:, u, 0:n],
                 in0=acc,
-                scalar=c_vec[:, u, ROW_FORM + CG + cg : ROW_FORM + CG + cg + 1],
+                scalar=c_vec[:, u, ROW_FORM + C_GROUPS + cg : ROW_FORM + C_GROUPS + cg + 1],
                 in1=first_term[grp, u][:, 0:n],
                 op0=MULT,
                 op1=ADD,
             )
 
-        def pack_y(grp, scalar_halves=()):
-            first, n, cg = groups[grp]
-            y_packed[grp] = work.tile([P, W, T], BF16, name="packed", align_bytes=64, bufs=4)
-            interleave(y_packed[grp][:, 0:n, :], y_rows[grp][:, :, 0:n], scalar_halves)
+        def both_kinds(grp, u):
+            kind0(grp, u)
+            kind1(grp, u)
+
+        def pack_y(grp, scalar_half=None):
+            n = GROUPS[grp][1]
+            y_packed[grp] = new_packed()
+            pack_rows(y_packed[grp][:, 0:n, :], y_rows[grp][:, :, 0:n], scalar_half)
 
         def quantize_y(grp):
-            first, n, cg = groups[grp]
-            y_codes = work.tile([P, W], U32, name="y_codes", align_bytes=64, bufs=3)
-            nc.vector.quantize_mx(
-                out=y_codes[:, 0:n].bitcast(FP8X4),
-                scales=y_scales[:, cg, first : first + n],
-                in_=y_packed[grp][:, 0:n, :].rearrange("p i t -> p (i t)"),
-            )
+            first, n, cg = GROUPS[grp]
+            y_codes = work.tile([P, W], U32, name="y_codes", align_bytes=ALIGN, bufs=Y_CODES_BUFS)
+            quantize(y_codes[:, 0:n], y_scales[:, cg, first : first + n], y_packed[grp][:, 0:n, :])
             nc.sync.dma_start(
                 out=out_1[cg, :, first : first + n, :].rearrange("p m t -> p (m t)").bitcast(I32),
                 in_=y_codes[:, 0:n].bitcast(I32),
             )
-            if first + n == S and cg > 0:
-                done = slice(0, CG - 1) if cg < CG - 1 else slice(CG - 1, CG)
-                for quad in range(4):
-                    nc.sync.dma_start(
-                        out=out_2[done, 4 * quad : 4 * quad + 4, :].rearrange("g r m -> r g m").bitcast(I32),
-                        in_=y_scales[32 * quad : 32 * quad + 4, done, :].bitcast(I32),
-                    )
 
-        def turn_y(grp, blocks):
-            for b in blocks:
-                turned[grp, b] = bank()
-                for u in range(T):
-                    nc.tensor.transpose(
-                        turned[grp, b][:, P * u : P * (u + 1)], y_rows[grp][:, u, P * b : P * (b + 1)], ident[:]
-                    )
+        def store_y_scales(c_groups):
+            for quad in range(QUADRANTS):
+                nc.sync.dma_start(
+                    out=out_2[c_groups, 4 * quad : 4 * quad + 4, :].rearrange("g r m -> r g m").bitcast(I32),
+                    in_=y_scales[32 * quad : 32 * quad + 4, c_groups, :].bitcast(I32),
+                )
 
-        def store_y(grp, blocks, on_vector=()):
-            first, n, cg = groups[grp]
+        def store_y(grp, blocks, vector_blocks=()):
+            first, cg = GROUPS[grp][0], GROUPS[grp][2]
             for b in blocks:
-                y_out = work.tile([P, W], F32, name="y_out", align_bytes=64, bufs=8)
-                dst = y_out[:].rearrange("i (m u) -> i m u", u=T)
-                src = turned[grp, b][:].rearrange("i (u m) -> i m u", u=T)
-                if b in on_vector:
+                turned = next_bank(F32)
+                for u in range(SLOTS):
+                    nc.tensor.transpose(turned[:, P * u : P * (u + 1)], y_rows[grp][:, u, P * b : P * (b + 1)], ident[:])
+                y_out = work.tile([P, W], F32, name="y_out", align_bytes=ALIGN, bufs=Y_OUT_BUFS)
+                dst = y_out[:].rearrange("i (m u) -> i m u", u=SLOTS)
+                src = turned[:].rearrange("i (u m) -> i m u", u=SLOTS)
+                if b in vector_blocks:
                     nc.vector.tensor_copy(out=dst, in_=src)
                 else:
                     nc.scalar.copy(out=dst, in_=src)
                 nc.sync.dma_start(out=out_0[first + P * b : first + P * (b + 1), W * cg : W * (cg + 1)], in_=y_out[:])
 
-        def emit_y(grp, blocks, on_vector=()):
-            turn_y(grp, blocks)
-            store_y(grp, blocks, on_vector)
 
-        order_modes(0)
-        order_modes(1)
+        regroup(modes_sb, modes_in, 0, 2)
+        regroup(modes_scales_sb, modes_scales_in, 0, 1)
+        regroup(modes_scales_sb, modes_scales_in, 1, 1)
         pack_sinc(0, 0)
-        order_modes(2)
-        order_modes(3)
+        regroup(modes_sb, modes_in, 1, 2)
         pack_sinc(0, 1)
         quantize_sinc(0, 0)
-        for w in range(0, 8):
-            weights(0, w)
+        for step in range(0, 8):
+            pair_weights(0, step)
         pack_h(0, 0)
         quantize_sinc(0, 1)
         quantize_h(0, 0)
         pack_h(0, 1)
-        for w in range(8, 13):
-            weights(0, w, w == 10)
-        turn_c_rows()
+        for step in range(8, 13):
+            pair_weights(0, step, on_vector=step == 10)
+        turn_c_vec()
+        for step in range(13, 16):
+            pair_weights(0, step, on_vector=step == 13)
         quantize_h(0, 1)
-        for w in range(13, 16):
-            weights(0, w, w == 13)
+        pair_weights(1, 0)
         pack_h(0, 2)
-        weights(1, 0)
-        pack_h(0, 3, (1,))
+        pack_h(0, 3, SECOND_HALF)
         quantize_h(0, 2)
         quantize_h(0, 3)
+        for step in range(1, 5):
+            pair_weights(1, step)
+
+        kind0(0, 0)
+        pair_weights(1, 5)
+        pair_weights(1, 6)
+        kind0(0, 1)
+        kind0(0, 2)
+        pair_weights(1, 7)
+        kind0(0, 3)
         pack_sinc(1, 0)
         pack_sinc(1, 1)
         quantize_sinc(1, 0)
-        weights(1, 1)
-        weights(1, 2)
-        kind0(0, 0)
-        weights(1, 3)
-        kind0(0, 1)
-        kind0(0, 2)
-        weights(1, 4)
-        kind1(0, 0)
         quantize_sinc(1, 1)
-        kind0(0, 3)
-        weights(1, 5)
-        kind1(0, 1)
-        kind1(0, 2)
-        for w in range(6, 9):
-            weights(1, w)
+        kind1(0, 0)
         pack_sinc(2, 0)
-        pack_sinc(2, 1, (1,))
-        kind1(0, 3)
-        kind0(1, 0)
-        kind1(1, 0)
+        for u in range(1, SLOTS):
+            kind1(0, u)
+        pair_weights(1, 8)
+        both_kinds(1, 0)
+        pack_sinc(2, 1, SECOND_HALF)
+        kind0(1, 1)
+        pair_weights(1, 9)
+        kind1(1, 1)
+        kind0(1, 2)
         quantize_sinc(2, 0)
         quantize_sinc(2, 1)
-        weights(1, 9)
-        for u in (1, 2):
-            kind0(1, u)
-            kind1(1, u)
-        for w in range(10, 13):
-            weights(1, w)
+        pair_weights(1, 10)
+        kind1(1, 2)
+        pair_weights(1, 11)
+        both_kinds(1, 3)
         pack_h(1, 0)
-        kind0(1, 3)
-        kind1(1, 3)
-        weights(1, 13)
-        weights(1, 14)
-        pack_h(1, 1)
+        pair_weights(1, 12)
+        pair_weights(1, 13, on_vector=True)
+        pack_h(1, 1, SECOND_HALF)
         pack_h(1, 2)
+        pair_weights(1, 14)
+        store_y(0, (0, 1))
+        both_kinds(2, 0)
         quantize_h(1, 0)
         quantize_h(1, 1)
-        emit_y(0, range(4))
-        weights(1, 15)
-        kind0(2, 0)
-        kind1(2, 0)
-        quantize_h(1, 2)
         kind0(2, 1)
+        kind0(2, 2)
+        pair_weights(1, 15)
+        store_y(0, (2, 3))
+        kind0(2, 3)
         kind1(2, 1)
-        pack_h(1, 3, (0, 1))
-        kind0(2, 2, True)
-        kind0(2, 3, True)
-        emit_y(1, range(4))
-        kind0(3, 0, True)
-        quantize_h(1, 3)
-        pack_y(0, (1,))
         kind1(2, 2)
+        pack_h(1, 3)
+        quantize_h(1, 2)
+        quantize_h(1, 3)
+        store_y(1, (0, 1))
         kind1(2, 3)
-        kind0(3, 1)
+
+        pack_y(0, SECOND_HALF)
+        kind0(3, 0, on_vector=True)
+        store_y(1, (2, 3))
+        pack_y(1, FIRST_HALF)
+        kind0(3, 1, on_vector=True)
         kind0(3, 2)
+        kind0(3, 3)
+        kind0(4, 0)
         kind1(3, 0)
-        kind0(3, 3, True)
-        pack_y(1, (0,))
-        for u in range(1, 4):
-            kind1(3, u)
-        emit_y(2, range(4), (1,))
-        pack_y(2)
-        for u in range(3):
-            quantize_y(u)
-            kind0(4, u)
-            if u == 2:
-                pack_y(3, (0,))
-            kind1(4, u)
+        kind0(4, 1)
+        quantize_y(0)
+        kind1(3, 1)
+        kind1(3, 2)
+        store_y(2, (0, 1))
+        pack_y(2, FIRST_HALF)
+        kind0(4, 2, on_vector=True)
+        kind1(3, 3)
         kind0(4, 3)
+        quantize_y(1)
+        store_y(2, (2, 3))
+        kind1(4, 0)
+        quantize_y(2)
+        kind1(4, 1)
+        store_y(3, (0, 1), vector_blocks=(0,))
+        kind1(4, 2)
         kind1(4, 3)
-        emit_y(3, range(4))
+        pack_y(3, FIRST_HALF)
+
+        kind0(5, 0, on_vector=True)
+        store_y(3, (2, 3))
         quantize_y(3)
-        pack_y(4)
-        for u in range(3):
-            kind0(5, u)
+        kind0(5, 1)
+        kind0(5, 2, on_vector=True)
+        pack_y(4, SECOND_HALF)
+        kind0(5, 3, on_vector=True)
         kind1(5, 0)
+        store_y(4, (0, 1))
         quantize_y(4)
-        kind0(5, 3)
+        store_y_scales(slice(0, C_GROUPS - 1))
         kind1(5, 1)
-        kind0(6, 0)
-        kind0(6, 1)
         kind1(5, 2)
+        kind0(6, 0)
         kind1(5, 3)
-        turn_y(4, range(4))
-        store_y(4, range(3))
+        store_y(4, (2, 3))
         pack_y(5)
-        quantize_y(5)
-        turn_y(5, (0,))
-        kind0(6, 2)
         kind1(6, 0)
-        kind0(6, 3, True)
+        quantize_y(5)
+        kind0(6, 1)
+        kind0(6, 2)
+        kind0(6, 3)
         kind1(6, 1)
-        kind1(6, 2)
-        store_y(4, (3,))
         store_y(5, (0,))
+        kind1(6, 2)
         kind1(6, 3)
-        emit_y(5, (1,), (1,))
+        store_y(5, (1,))
         pack_y(6)
-        emit_y(6, range(2))
+        store_y(6, (0,))
         quantize_y(6)
+        store_y_scales(slice(C_GROUPS - 1, C_GROUPS))
+        store_y(6, (1,))

from contextlib import ExitStack

import concourse.mybir as mybir
from concourse.masks import make_identity

SAMPLES, KINDS, MODES, DISTANCES, VECTORS = 1024, 2, 512, 1024, 1536
FLOPS = 2 * SAMPLES * MODES * KINDS * DISTANCES + 2 * SAMPLES * KINDS * DISTANCES * VECTORS

F32 = mybir.dt.float32
BF16 = mybir.dt.bfloat16
I32 = mybir.dt.int32
U32 = mybir.dt.uint32
U8 = mybir.dt.uint8
FP8X4 = mybir.dt.float8_e4m3fn_x4
FP4X4 = mybir.dt.float4_e2m1fn_x4
IDENTITY = mybir.ActivationFunctionType.Identity
MULT = mybir.AluOpType.mult
ADD = mybir.AluOpType.add

P = 128
SLOTS = 4
RUN = 8
W = P * SLOTS
QUADRANTS = 4
ALIGN = 64
CHUNKS = SAMPLES // W
D_PASSES = DISTANCES // W
H_TILES = KINDS * D_PASSES
C_GROUPS = VECTORS // W

ROW_GAIN, ROW_BASE, D_ROWS = 0, H_TILES, 2 * H_TILES
ROW_FORM, ROW_SELF, C_ROWS = 0, KINDS * C_GROUPS, (KINDS + 1) * C_GROUPS

GROUPS = [(W * ch, W, cg) for ch in range(CHUNKS) for cg in range(C_GROUPS)][:-1] + [
    (SAMPLES - W, W // 2, C_GROUPS - 1),
    (SAMPLES - W // 2, W // 2, C_GROUPS - 1),
]

BANKS = 8
H_ROWS_BUFS, PACKED_BUFS, FIRST_TERM_BUFS, Y_ROWS_BUFS, Y_CODES_BUFS, Y_OUT_BUFS = 4, 4, 5, 6, 3, 8

FIRST_HALF, SECOND_HALF = 0, 1


def tile_powder_pattern_sinc_k5_kernel(
    tc, coef_words, coef_scales, modes_words, modes_scales, gain, base, sinc, form, selfscat, out_0, out_1, out_2
):
    nc = tc.nc
    with ExitStack() as ctx:
        keep = ctx.enter_context(tc.tile_pool(name="keep", bufs=1))
        work = ctx.enter_context(tc.tile_pool(name="work", bufs=1))
        psum = ctx.enter_context(tc.psum_pool(name="psum", bufs=BANKS))
        ctx.enter_context(tc.manual_schedule())

        def next_bank(dtype):
            return psum.tile([P, W], dtype, name="bank")

        coef_sb = keep.tile([P, 2 * SAMPLES], U8, align_bytes=ALIGN)
        modes_in = keep.tile([P, 2 * KINDS * DISTANCES], U8, align_bytes=ALIGN)
        modes_sb = keep.tile([P, 2 * KINDS * DISTANCES], U8, align_bytes=ALIGN)
        coef_scales_sb = keep.tile([P, SAMPLES], U8, align_bytes=ALIGN)
        modes_scales_in = keep.tile([P, KINDS * DISTANCES], U8, align_bytes=ALIGN)
        modes_scales_sb = keep.tile([P, KINDS * DISTANCES], U8, align_bytes=ALIGN)
        sinc_rows = keep.tile([P, C_GROUPS, D_PASSES, SLOTS, W], BF16, align_bytes=ALIGN)
        sinc_codes = keep.tile([P, C_GROUPS, D_PASSES, W], U32, align_bytes=ALIGN)
        sinc_scales = keep.tile([P, C_GROUPS, D_PASSES, W], U8, align_bytes=ALIGN)
        h_codes = keep.tile([P, CHUNKS, H_TILES, W], U32, align_bytes=ALIGN)
        h_scales = keep.tile([P, CHUNKS, H_TILES, W], U8, align_bytes=ALIGN)
        y_scales = keep.tile([P, C_GROUPS, SAMPLES], U8, align_bytes=ALIGN)
        d_vec_in = keep.tile([P, W], BF16, align_bytes=ALIGN)
        d_vec_rows = keep.tile([P, SLOTS, P], F32, align_bytes=ALIGN)
        d_vec = keep.tile([P, SLOTS, D_ROWS], F32, align_bytes=ALIGN)
        c_vec_in = keep.tile([P, W], BF16, align_bytes=ALIGN)
        c_vec = keep.tile([P, SLOTS, C_ROWS], F32, align_bytes=ALIGN)
        ident = keep.tile([P, P], F32, align_bytes=ALIGN)
        ident_bf16 = keep.tile([P, P], BF16, align_bytes=ALIGN)

        nc.vector.memset(modes_scales_in[:].bitcast(I32), 0)
        nc.vector.memset(coef_scales_sb[:].bitcast(I32), 0)
        nc.vector.memset(d_vec_rows[:], 0.0)
        nc.vector.memset(c_vec_in[:], 0.0)
        make_identity(nc, ident[:])
        nc.scalar.activation(out=ident_bf16[:], in_=ident[:], func=IDENTITY)
        nc.gpsimd.dma_start(out=c_vec_in[ROW_FORM:ROW_SELF, :], in_=form.rearrange("a (g n) -> (a g) n", n=W))
        nc.gpsimd.dma_start(out=c_vec_in[ROW_SELF:C_ROWS, :], in_=selfscat.rearrange("(g n) -> g n", n=W))

        def load_words(dst, src, first_column, columns):
            span = slice(2 * first_column, 2 * (first_column + columns))
            nc.sync.dma_start(out=dst[:, span].bitcast(I32), in_=src[0, :, span].bitcast(I32))

        def load_scales(dst, src):
            for quad in range(QUADRANTS):
                nc.sync.dma_start(
                    out=dst[32 * quad : 32 * quad + 4, :].bitcast(I32), in_=src[0, 4 * quad : 4 * quad + 4, :].bitcast(I32)
                )

        def load_sinc(cg, g):
            rows = sinc[W * g : W * (g + 1), W * cg : W * (cg + 1)].rearrange("(q t r) c -> t q r c", t=SLOTS, r=RUN)
            for t in range(SLOTS):
                nc.sync.dma_start(out=sinc_rows[:, cg, g, t, :], in_=rows[t])

        load_words(modes_in, modes_words, 0, DISTANCES)
        load_words(coef_sb, coef_words, 0, W)
        nc.sync.dma_start(out=d_vec_in[ROW_GAIN:ROW_BASE, :], in_=gain.rearrange("(j n) -> j n", n=W))
        nc.sync.dma_start(out=d_vec_in[ROW_BASE:D_ROWS, :], in_=base.rearrange("(j n) -> j n", n=W))
        load_scales(modes_scales_in, modes_scales)
        load_scales(coef_scales_sb, coef_scales)
        load_sinc(0, 0)
        load_words(modes_in, modes_words, DISTANCES, DISTANCES)
        load_sinc(0, 1)
        load_words(coef_sb, coef_words, W, W)
        for cg in range(1, C_GROUPS):
            for g in range(D_PASSES):
                load_sinc(cg, g)

        nc.vector.tensor_copy(
            out=d_vec_rows[0:D_ROWS, :, :].rearrange("j t (q r) -> j t q r", r=RUN),
            in_=d_vec_in[0:D_ROWS, :].rearrange("j (q t r) -> j t q r", t=SLOTS, r=RUN),
        )
        d_turned = next_bank(F32)
        for t in range(SLOTS):
            nc.tensor.transpose(d_turned[:, P * t : P * (t + 1)], d_vec_rows[:, t, :], ident[:])
        nc.scalar.activation(
            out=d_vec[:], in_=d_turned[:].rearrange("p (t j) -> p t j", t=SLOTS)[:, :, 0:D_ROWS], func=IDENTITY
        )

        def turn_c_vec():
            c_turned = next_bank(BF16)
            for u in range(SLOTS):
                nc.tensor.transpose(c_turned[:, P * u : P * (u + 1)], c_vec_in[:, u:W:SLOTS], ident_bf16[:])
            nc.scalar.activation(
                out=c_vec[:], in_=c_turned[:].rearrange("p (u j) -> p u j", u=SLOTS)[:, :, 0:C_ROWS], func=IDENTITY
            )

        def regroup(dst, src, kind, column_bytes):
            span = slice(column_bytes * DISTANCES * kind, column_bytes * DISTANCES * (kind + 1))
            run_words = RUN * column_bytes // 4
            nc.vector.tensor_copy(
                out=dst[:, span].bitcast(I32).rearrange("p (t b w) -> p t b w", t=SLOTS, w=run_words),
                in_=src[:, span].bitcast(I32).rearrange("p (b t w) -> p t b w", t=SLOTS, w=run_words),
            )

        h_rows, h_packed, sinc_packed = {}, {}, {}
        first_term, y_rows, y_packed = {}, {}, {}

        def scale_and_shift(dst, src, scale_col, shift_col, on_vector):
            if on_vector:
                nc.vector.tensor_scalar(dst, src, scale_col, shift_col, MULT, ADD)
            else:
                nc.scalar.activation(out=dst, in_=src, func=IDENTITY, scale=scale_col, bias=shift_col)

        def pair_weights(ch, step, on_vector=False):
            j, t = divmod(step, SLOTS)
            acc = next_bank(F32)
            kind, g = divmod(j, D_PASSES)
            col = DISTANCES * kind + DISTANCES // SLOTS * t + P * g
            nc.tensor.matmul_mx(
                out=acc[:],
                lhsT=modes_sb[:, 2 * col : 2 * (col + P)].bitcast(FP4X4),
                lhsT_scale=modes_scales_sb[:, col : col + P],
                rhs=coef_sb[:, 2 * W * ch : 2 * W * (ch + 1)].bitcast(FP4X4),
                rhs_scale=coef_scales_sb[:, W * ch : W * (ch + 1)],
                start=True,
                stop=True,
            )
            if t == 0:
                h_rows[ch, j] = work.tile([P, SLOTS, W], BF16, name="h_rows", align_bytes=ALIGN, bufs=H_ROWS_BUFS)
            gain_col = d_vec[:, t, ROW_GAIN + j : ROW_GAIN + j + 1]
            base_col = d_vec[:, t, ROW_BASE + j : ROW_BASE + j + 1]
            scale_and_shift(h_rows[ch, j][:, t, :], acc[:], gain_col, base_col, on_vector)

        def new_packed():
            return work.tile([P, W, SLOTS], BF16, name="packed", align_bytes=ALIGN, bufs=PACKED_BUFS)

        def pack(dst, src, walk, scalar_half):
            if scalar_half is None:
                nc.vector.tensor_copy(out=dst.rearrange(walk), in_=src.rearrange(walk))
                return
            half = dst.shape[1] // 2
            for k in range(2):
                span = slice(half * k, half * (k + 1))
                if k == scalar_half:
                    nc.scalar.copy(out=dst[:, span].rearrange(walk), in_=src[:, span].rearrange(walk))
                else:
                    nc.vector.tensor_copy(out=dst[:, span].rearrange(walk), in_=src[:, span].rearrange(walk))

        def pack_rows(packed, rows, scalar_half):
            pack(
                packed.rearrange("p (c i) t -> p c i t", i=4),
                rows.rearrange("p t (c i) -> p c i t", i=4),
                "p c i t -> p c t i",
                scalar_half,
            )

        def quantize(codes, scales, packed):
            nc.vector.quantize_mx(out=codes.bitcast(FP8X4), scales=scales, in_=packed.rearrange("p i t -> p (i t)"))

        def pack_h(ch, j, scalar_half=None):
            h_packed[ch, j] = new_packed()
            pack_rows(h_packed[ch, j][:], h_rows[ch, j][:], scalar_half)

        def quantize_h(ch, j):
            quantize(h_codes[:, ch, j, :], h_scales[:, ch, j, :], h_packed[ch, j][:])

        def pack_sinc(cg, g, scalar_half=None):
            sinc_packed[cg, g] = new_packed()
            pack(
                sinc_packed[cg, g][:].rearrange("p (u m) t -> p u m t", u=SLOTS),
                sinc_rows[:, cg, g, :, :].rearrange("p t (m u) -> p u m t", u=SLOTS),
                "p u m t -> p m t u",
                scalar_half,
            )

        def quantize_sinc(cg, g):
            quantize(sinc_codes[:, cg, g, :], sinc_scales[:, cg, g, :], sinc_packed[cg, g][:])

        def partial_pattern(grp, u, kind):
            first, n, cg = GROUPS[grp]
            ch, lo = divmod(first, W)
            acc = next_bank(F32)
            for g in range(D_PASSES):
                nc.tensor.matmul_mx(
                    out=acc[:, 0:n],
                    lhsT=sinc_codes[:, cg, g, P * u : P * (u + 1)].bitcast(FP8X4),
                    lhsT_scale=sinc_scales[:, cg, g, P * u : P * (u + 1)],
                    rhs=h_codes[:, ch, D_PASSES * kind + g, lo : lo + n].bitcast(FP8X4),
                    rhs_scale=h_scales[:, ch, D_PASSES * kind + g, lo : lo + n],
                    start=(g == 0),
                    stop=(g == D_PASSES - 1),
                )
            return acc[:, 0:n]

        def kind0(grp, u, on_vector=False):
            n, cg = GROUPS[grp][1:]
            acc = partial_pattern(grp, u, 0)
            first_term[grp, u] = work.tile([P, W], F32, name="first_term", align_bytes=ALIGN, bufs=FIRST_TERM_BUFS)
            form_col = c_vec[:, u, ROW_FORM + cg : ROW_FORM + cg + 1]
            self_col = c_vec[:, u, ROW_SELF + cg : ROW_SELF + cg + 1]
            scale_and_shift(first_term[grp, u][:, 0:n], acc, form_col, self_col, on_vector)

        def kind1(grp, u):
            n, cg = GROUPS[grp][1:]
            acc = partial_pattern(grp, u, 1)
            if u == 0:
                y_rows[grp] = work.tile([P, SLOTS, W], F32, name="y_rows", align_bytes=ALIGN, bufs=Y_ROWS_BUFS)
            nc.vector.scalar_tensor_tensor(
                out=y_rows[grp][:, u, 0:n],
                in0=acc,
                scalar=c_vec[:, u, ROW_FORM + C_GROUPS + cg : ROW_FORM + C_GROUPS + cg + 1],
                in1=first_term[grp, u][:, 0:n],
                op0=MULT,
                op1=ADD,
            )

        def both_kinds(grp, u):
            kind0(grp, u)
            kind1(grp, u)

        def pack_y(grp, scalar_half=None):
            n = GROUPS[grp][1]
            y_packed[grp] = new_packed()
            pack_rows(y_packed[grp][:, 0:n, :], y_rows[grp][:, :, 0:n], scalar_half)

        def quantize_y(grp):
            first, n, cg = GROUPS[grp]
            y_codes = work.tile([P, W], U32, name="y_codes", align_bytes=ALIGN, bufs=Y_CODES_BUFS)
            quantize(y_codes[:, 0:n], y_scales[:, cg, first : first + n], y_packed[grp][:, 0:n, :])
            nc.sync.dma_start(
                out=out_1[cg, :, first : first + n, :].rearrange("p m t -> p (m t)").bitcast(I32),
                in_=y_codes[:, 0:n].bitcast(I32),
            )

        def store_y_scales(c_groups):
            for quad in range(QUADRANTS):
                nc.sync.dma_start(
                    out=out_2[c_groups, 4 * quad : 4 * quad + 4, :].rearrange("g r m -> r g m").bitcast(I32),
                    in_=y_scales[32 * quad : 32 * quad + 4, c_groups, :].bitcast(I32),
                )

        def store_y(grp, blocks, vector_blocks=()):
            first, cg = GROUPS[grp][0], GROUPS[grp][2]
            for b in blocks:
                turned = next_bank(F32)
                for u in range(SLOTS):
                    nc.tensor.transpose(turned[:, P * u : P * (u + 1)], y_rows[grp][:, u, P * b : P * (b + 1)], ident[:])
                y_out = work.tile([P, W], F32, name="y_out", align_bytes=ALIGN, bufs=Y_OUT_BUFS)
                dst = y_out[:].rearrange("i (m u) -> i m u", u=SLOTS)
                src = turned[:].rearrange("i (u m) -> i m u", u=SLOTS)
                if b in vector_blocks:
                    nc.vector.tensor_copy(out=dst, in_=src)
                else:
                    nc.scalar.copy(out=dst, in_=src)
                nc.sync.dma_start(out=out_0[first + P * b : first + P * (b + 1), W * cg : W * (cg + 1)], in_=y_out[:])


        regroup(modes_sb, modes_in, 0, 2)
        regroup(modes_scales_sb, modes_scales_in, 0, 1)
        regroup(modes_scales_sb, modes_scales_in, 1, 1)
        pack_sinc(0, 0)
        regroup(modes_sb, modes_in, 1, 2)
        pack_sinc(0, 1)
        quantize_sinc(0, 0)
        for step in range(0, 8):
            pair_weights(0, step)
        pack_h(0, 0)
        quantize_sinc(0, 1)
        quantize_h(0, 0)
        pack_h(0, 1)
        for step in range(8, 13):
            pair_weights(0, step, on_vector=step == 10)
        turn_c_vec()
        for step in range(13, 16):
            pair_weights(0, step, on_vector=step == 13)
        quantize_h(0, 1)
        pair_weights(1, 0)
        pack_h(0, 2)
        pack_h(0, 3, SECOND_HALF)
        quantize_h(0, 2)
        quantize_h(0, 3)
        for step in range(1, 5):
            pair_weights(1, step)

        kind0(0, 0)
        pair_weights(1, 5)
        pair_weights(1, 6)
        kind0(0, 1)
        kind0(0, 2)
        pair_weights(1, 7)
        kind0(0, 3)
        pack_sinc(1, 0)
        pack_sinc(1, 1)
        quantize_sinc(1, 0)
        quantize_sinc(1, 1)
        kind1(0, 0)
        pack_sinc(2, 0)
        for u in range(1, SLOTS):
            kind1(0, u)
        pair_weights(1, 8)
        both_kinds(1, 0)
        pack_sinc(2, 1, SECOND_HALF)
        kind0(1, 1)
        pair_weights(1, 9)
        kind1(1, 1)
        kind0(1, 2)
        quantize_sinc(2, 0)
        quantize_sinc(2, 1)
        pair_weights(1, 10)
        kind1(1, 2)
        pair_weights(1, 11)
        both_kinds(1, 3)
        pack_h(1, 0)
        pair_weights(1, 12)
        pair_weights(1, 13, on_vector=True)
        pack_h(1, 1, SECOND_HALF)
        pack_h(1, 2)
        pair_weights(1, 14)
        store_y(0, (0, 1))
        both_kinds(2, 0)
        quantize_h(1, 0)
        quantize_h(1, 1)
        kind0(2, 1)
        kind0(2, 2)
        pair_weights(1, 15)
        store_y(0, (2, 3))
        kind0(2, 3)
        kind1(2, 1)
        kind1(2, 2)
        pack_h(1, 3)
        quantize_h(1, 2)
        quantize_h(1, 3)
        store_y(1, (0, 1))
        kind1(2, 3)

        pack_y(0, SECOND_HALF)
        kind0(3, 0, on_vector=True)
        store_y(1, (2, 3))
        pack_y(1, FIRST_HALF)
        kind0(3, 1, on_vector=True)
        kind0(3, 2)
        kind0(3, 3)
        kind0(4, 0)
        kind1(3, 0)
        kind0(4, 1)
        quantize_y(0)
        kind1(3, 1)
        kind1(3, 2)
        store_y(2, (0, 1))
        pack_y(2, FIRST_HALF)
        kind0(4, 2, on_vector=True)
        kind1(3, 3)
        kind0(4, 3)
        quantize_y(1)
        store_y(2, (2, 3))
        kind1(4, 0)
        quantize_y(2)
        kind1(4, 1)
        store_y(3, (0, 1), vector_blocks=(0,))
        kind1(4, 2)
        kind1(4, 3)
        pack_y(3, FIRST_HALF)

        kind0(5, 0, on_vector=True)
        store_y(3, (2, 3))
        quantize_y(3)
        kind0(5, 1)
        kind0(5, 2, on_vector=True)
        pack_y(4, SECOND_HALF)
        kind0(5, 3, on_vector=True)
        kind1(5, 0)
        store_y(4, (0, 1))
        quantize_y(4)
        store_y_scales(slice(0, C_GROUPS - 1))
        kind1(5, 1)
        kind1(5, 2)
        kind0(6, 0)
        kind1(5, 3)
        store_y(4, (2, 3))
        pack_y(5)
        kind1(6, 0)
        quantize_y(5)
        kind0(6, 1)
        kind0(6, 2)
        kind0(6, 3)
        kind1(6, 1)
        store_y(5, (0,))
        kind1(6, 2)
        kind1(6, 3)
        store_y(5, (1,))
        pack_y(6)
        store_y(6, (0,))
        quantize_y(6)
        store_y_scales(slice(C_GROUPS - 1, C_GROUPS))
        store_y(6, (1,))
